import numpy as np, ml_dtypes
CORES = [16,18,20,22]
N = 4
import mx_ref
BF = ml_dtypes.bfloat16
def entries(a):
    return np.ascontiguousarray(a.T).reshape(-1)
def table(e):
    return np.ascontiguousarray(np.reshape(e, (-1, 16)).T).astype(np.int32)
def cols(t, e):
    v = np.concatenate([t.reshape(128, -1, 4), np.zeros((128, 1, 4), BF)], axis=1)
    return np.ascontiguousarray(v[:, e]).reshape(128, -1)
def cut(t, i, w=512):
    return t[:, w * i:w * i + w]
def f(rng, *shape):
    return mx_ref.flush((rng.standard_normal(shape, dtype=np.float32) * np.exp2(rng.integers(-2, 3, shape[:-1] + (1,)))).astype(BF))
def wide(rng, *shape, cols=0):
    v = rng.standard_normal(shape, dtype=np.float32) * np.exp2(rng.integers(-12, 13, shape)).astype(np.float32)
    if cols: v *= np.repeat(np.exp2(rng.integers(-cols, cols + 1, shape[:-2] + (1, shape[-1] // 4))) * (rng.random(shape[:-2] + (1, shape[-1] // 4)) > 0.0625), 4, axis=-1).astype(np.float32)
    return mx_ref.flush(v.astype(BF))
T, CAPP, F = 128, 160, 8
def inverse(e):
    o = np.full(F * T, -1)
    k = np.flatnonzero(e >= 0); k = k[np.argsort(e[k], kind="stable")]; v = e[k]
    at = np.arange(len(k)) - np.searchsorted(v, v); keep = at < F
    o[(F * v + at)[keep]] = k[keep]
    return o
def counts(rng, most=CAPP):
    n = np.zeros((N, N), int)
    for r in range(N):
        a = rng.integers(T // N, 4 * T // N + 1, N)
        n[:, r] = a + np.bincount(rng.permutation(np.repeat(np.arange(N), most - a))[:4 * T - a.sum()], minlength=N)
    return n
def senders(rng, n):
    return np.stack([rng.permutation(np.repeat(np.arange(N), n[:, r])) for r in range(N)])
def lists(rng, A, node=None, top=None, popular=False, big=None):
    sn = np.full((N, N * CAPP), -1); nb = np.zeros((N, 4 * T), int)
    for s in range(N):
        d, e = np.nonzero(A == s); free = rng.permutation(T)
        if node is not None: v = node[d, e]
        elif top is not None:
            t = top[d, e]; h = (t.sum() + F - 1) // F; v = np.zeros(len(d), int); big.append(free[:h])
            v[t] = rng.permutation(np.repeat(free[:h], F))[:t.sum()]
            v[~t] = rng.permutation(np.repeat(free[h:], F))[:(~t).sum()]
        else:
            h = len(d) // 16 if popular else 0
            v = rng.permutation(np.concatenate([np.repeat(free[:h], F), rng.permutation(np.repeat(free[h:], F))[:len(d) - F * h]]))
        for q in range(N):
            k = np.flatnonzero(d == q); c = rng.permutation(CAPP)[:len(k)]
            sn[s, q * CAPP + c] = v[k]; nb[q, e[k]] = s * CAPP + c
    return {"sn": np.stack([table(a) for a in sn]), "nb": np.stack([table(a) for a in nb]), "il": np.stack([table(inverse(a)) for a in sn])}
def setup_inputs(rng):
    return {"x": f(rng, N, 128, 4 * T), "gr": f(rng, N, 128, 4 * T), "w": np.repeat(f(rng, 1, 128, 2048), N, axis=0), "w2": np.repeat(f(rng, 1, 128, 2048), N, axis=0), **lists(rng, senders(rng, counts(rng)))}
def setup_inputs_ties(rng):
    d = setup_inputs(rng); own = d["x"].reshape(N, 128, T, 4)
    d["x"] = np.ascontiguousarray(np.where(rng.random((N, 1, T, 1)) < 0.7, own[:1], own)).reshape(N, 128, 4 * T)
    n = counts(rng, min(CAPP, T)); A = np.zeros((N, 4 * T), int); node = np.zeros((N, 4 * T), int)
    e = np.arange(4 * T); j = e % T; k = (e // T + j) % 4
    for r in range(N):
        o = rng.permutation(N); to = 4 * rng.permutation(T)[j] + k
        A[r, to] = np.repeat(o, n[o, r]); node[r, to] = rng.permutation(T)[j]
    return {**d, **lists(rng, A, node=node)}
def setup_inputs_oneside(rng):
    d = setup_inputs(rng); top = np.zeros((N, 4 * T), bool); big = []
    for r in range(N): top[r, 4 * rng.permutation(T)[:T // 2] + 3] = True
    d.update(lists(rng, senders(rng, counts(rng)), top=top, big=big))
    v = np.abs(d["x"].astype(np.float32)).reshape(N, 128, T, 4)
    for s in range(N): v[s][:, big[s]] *= 64
    d["x"] = v.reshape(N, 128, 4 * T).astype(BF); d["w"] = np.abs(d["w"].astype(np.float32)).astype(BF)
    return d
def setup_inputs_popular(rng):
    return {**setup_inputs(rng), **lists(rng, senders(rng, counts(rng)), popular=True)}
def setup_inputs_full(rng):
    n = np.zeros((N, N), int); o = rng.permutation(N); at = rng.permutation(N)
    m = 4 * T // CAPP; rest = 4 * T - m * CAPP
    for r in range(N):
        for j in range(m): n[o[(at[r] + j) % N], r] = CAPP
        if rest: n[o[(at[r] + m) % N], r] = rest
    return {**setup_inputs(rng), **lists(rng, senders(rng, n))}
def setup_inputs_spread(rng):
    d = setup_inputs(rng); d["x"] = wide(rng, N, 128, 4 * T, cols=8); return d
def check_inputs(d):
    b = []
    for t in ("w", "w2"):
        if (d[t] != d[t][:1]).any(): b.append(t)
    e = np.stack([entries(a) for a in d["sn"]])
    if e.min() < -1 or e.max() >= T: b.append("sn")
    e = np.clip(e, -1, T - 1)
    for r in range(N):
        if np.bincount(e[r][e[r] >= 0], minlength=T).max() > F: b.append("sn")
        if not np.array_equal(np.sort(entries(d["nb"][r])), np.flatnonzero(e[:, r * CAPP:(r + 1) * CAPP].reshape(-1) >= 0)): b.append("nb")
        if not np.array_equal(entries(d["il"][r]), inverse(e[r])): b.append("il")
    return b
def four(v):
    return [mx_ref.quantize(np.ascontiguousarray(cut(v, b))) for b in range(4)]
def reference(x, gr, w, w2, sn, nb, il):
    G = []
    for r in range(N):
        arrived = mx_ref.quantize(np.concatenate([cols(x[s], entries(sn[s])[r * CAPP:(r + 1) * CAPP]) for s in range(N)], axis=1))
        e = entries(nb[r])
        z = [mx_ref.matmul(W, arrived)[:, e].reshape(128, T, 4) + np.float32(0.0) for W in four(w[r])]
        win = np.stack([v.argmax(axis=2) for v in z], axis=2)
        g = gr[r].reshape(128, T, 4); back = np.zeros((128, N * CAPP, 4), BF)
        for k in range(4): back[:, e[k::4]] = np.where(win == k, g, np.zeros_like(g))
        G.append(back)
    y = np.zeros((N, 128, 4 * T), np.float32)
    for s in range(N):
        q = mx_ref.quantize(np.concatenate([G[r][:, s * CAPP:(s + 1) * CAPP].reshape(128, -1) for r in range(N)], axis=1))
        e = entries(il[s])
        for b, V in enumerate(four(w2[s])):
            u = mx_ref.matmul(V, q); t = np.zeros((128, T), np.float32)
            for i in range(F):
                k = e[i::F]; has = k >= 0
                t[:, has] += u[:, k[has]]
            y[s][:, T * b:T * b + T] = t
    return {"y": y}

@@ -1,0 +1,418 @@
+import numpy as np
+from concourse.bass import DstId, RemoteDMATransfer
+from concourse.mybir import dt, AluOpType, ActivationFunctionType
+
+N, NODES, CAP, F = 4, 128, 160, 8
+SL = N * CAP
+HF = 2 * CAP
+UW = SL + 8
+TR = 3 * 2 * NODES
+ORDER = (0, 2, 1, 3)
+
+SCRATCH = {
+    "snl": ("sbuf", [128, SL // 16], "int32"), "nbl": ("sbuf", [128, 32], "int32"), "dnb": ("dram", [16, 32], "int32"),
+    "nbo": ("sbuf", [128, 32], "uint16"), "nbi": ("sbuf", [128, 32], "uint16"),
+    "ill": ("sbuf", [128, 64], "int32"), "ilo": ("sbuf", [128, 64], "uint16"), "dil": ("dram", [16, 64], "int32"),
+    "iln": ("sbuf", [128, 64], "int32"), "ilp": ("sbuf", [128, 64], "uint16"),
+    "glo": ("sbuf", [128, 32], "uint16"), "gio": ("sbuf", [128, 32], "int32"),
+    "pidx": ("sbuf", [128, 1], "int32"), "p12": ("sbuf", [128, 1], "int32"), "p3": ("sbuf", [128, 1], "int32"),
+    "p12f": ("sbuf", [128, 1], "float32"), "ppf": ("sbuf", [128, 1], "float32"),
+    "vals": ("sbuf", [128, 512], "int32"), "inv": ("sbuf", [128, SL], "int32"),
+    "iv": ("sbuf", [128, 40], "int32"), "lt": ("sbuf", [128, 40], "uint16"),
+    "xt": ("sbuf", [128, 512], "bfloat16"), "grt": ("sbuf", [128, 512], "bfloat16"),
+    "wt": ("sbuf", [128, 2048], "bfloat16"), "w2t": ("sbuf", [128, 2048], "bfloat16"),
+    "xg": ("sbuf", [128, 4 * SL], "bfloat16"), "gt": ("sbuf", [128, 4 * SL], "bfloat16"),
+    "d0": ("sbuf", [128, 4 * TR], "bfloat16"), "d1": ("sbuf", [128, 4 * TR], "bfloat16"),
+    "mk": ("sbuf", [128, TR], "bfloat16"), "gb": ("sbuf", [128, 8 * TR], "bfloat16"),
+    "rs": ("sbuf", [128, F * NODES], "float32"),
+    "uu": ("sbuf", [128, 4 * UW], "float32"),
+    "ps": ("psum", [128, 4096], "float32"),
+}
+for _i in range(4, 8):
+    SCRATCH["nb%d" % _i] = ("sbuf", [128, 32], "int32")
+for _n, _w in (("wq", 512), ("vq", 512), ("sx", SL), ("sg", SL), ("lx", SL), ("lg", SL)):
+    SCRATCH[_n + "c"] = ("sbuf", [128, _w], "float8_e4m3fn_x4")
+    SCRATCH[_n + "p"] = ("sbuf", [128, _w], "uint8")
+for _b in range(4):
+    SCRATCH["so%d" % _b] = ("sbuf", [128, SL // 16], "uint16")
+    SCRATCH["z%d" % _b] = ("sbuf", [128, SL], "float32")
+    SCRATCH["zs%d" % _b] = ("sbuf", [128, 256], "float32")
+    SCRATCH["mm%d" % _b] = ("sbuf", [128, 256], "float32")
+    if _b % 2:
+        SCRATCH["ug%d" % _b] = ("sbuf", [128, F * NODES], "float32")
+        SCRATCH["us%d" % _b] = ("sbuf", [128, F * NODES], "float32")
+    else:
+        for _k in range(4):
+            SCRATCH["ac%d%d" % (_b, _k)] = ("sbuf", [128, 256], "float32")
+    SCRATCH["yo%d" % _b] = ("sbuf", [128, 128], "float32")
+
+EVENTS = 144
+SEMAPHORES = ["ax0", "ax1", "ag0", "ag1", "sentx", "sentg"] + ["e%d" % _i for _i in range(EVENTS)]
+
+
+def rank_program(g, core, T, topo):
+    r = T.rank_of(core)
+    if r is None:
+        return
+    A, Act = AluOpType, ActivationFunctionType
+    cores = list(T.cores)
+    Q = {"g": g, "v": g.vector, "a": g.scalar, "s": g.sync, "t": g.tensor}
+    V, S, Y, TE = g.vector, g.scalar, g.sync, g.tensor
+
+    pair = r - r % 2
+    far = N // 2 - pair
+    mate = pair + 1 - r % 2
+    STAGES = ((mate,), (far, far + 1))
+    OWN, PART, NEAR, FAR = CAP * r, CAP * mate, CAP * pair, CAP * far
+
+    made, seen = [], set()
+
+    def ev():
+        e = {"k": len(made), "s": T.sem["e%d" % len(made)], "n": 0, "w": False}
+        made.append(e)
+        return e
+
+    def inc(op, e, n=1):
+        op.then_inc(e["s"], n)
+        e["n"] += n
+        return e
+
+    def do(op):
+        return inc(op, ev())
+
+    def need(q, *es):
+        for e in es:
+            if (q, e["k"]) not in seen:
+                seen.add((q, e["k"]))
+                e["w"] = True
+                Q[q].wait_ge(e["s"], e["n"])
+
+    def send(src, dst, stage, arrived, left):
+        for part in (0, 1):
+            tr = []
+            for i, d in enumerate(STAGES[stage]):
+                rid, pid, _ = topo.addr(cores[d])
+                es = topo.engines(cores[r], cores[d])[(part + i) % 2::2]
+                a, b = CAP * d, CAP * r
+                if part == 0:
+                    f, t = T[src + "c"][:, a:a + CAP].bitcast(dt.uint8), T[dst + "c"][:, b:b + CAP].bitcast(dt.uint8)
+                else:
+                    f, t = T[src + "p"][:, a:a + CAP], T[dst + "p"][:, b:b + CAP]
+                tr.append(RemoteDMATransfer(dst_ids=[DstId(rid=rid, pnc=pid)], dma_engine_mask=sum(1 << e for e in es),
+                                            remote_sem=arrived, src=f, dst=t))
+            g.remote_dma_fused(tr, local_sem=left)
+
+    arrive = [sum(len(topo.engines(cores[s], cores[r])) for s in st) for st in STAGES]
+    sent = sum(len(topo.engines(cores[r], cores[d])) for st in STAGES for d in st)
+
+    e_x, e_sn, e_w, e_dnb, e_nb, e_gr, e_inv, e_iln = ev(), ev(), ev(), ev(), ev(), ev(), ev(), ev()
+    inc(Y.dma_start(T.xt[:, :], T.x[:, :]), e_x, 16)
+    for p in range(4):
+        inc(Y.dma_start(T.snl[16 * p:16 * p + 16, :], T.sn[:, :]), e_sn, 16)
+    for p in range(4, 8):
+        inc(S.dma_start(T.snl[16 * p:16 * p + 16, :], T.sn[:, :]), e_sn, 16)
+    for i, k in enumerate(ORDER):
+        inc(S.dma_start(T.dnb[:, 8 * i:8 * i + 8], T.nb[k:16:4, :]), e_dnb, 16)
+    inc(S.dma_start(T.wt[:, :], T.w[:, :]), e_w, 16)
+    inc(Y.dma_start(T.grt[:, :], T.gr[:, :]), e_gr, 16)
+    inc(Y.dma_start(T.inv[0:1, :], T.sn[:, :]), e_inv, 16)
+    need("s", e_dnb)
+    for p in range(8):
+        inc(Y.dma_start(T.nbl[16 * p:16 * p + 16, :], T.dnb[:, :]), e_nb, 16)
+    for p in range(8):
+        inc(Y.dma_start(T.iln[16 * p:16 * p + 16, :], T.il[:, :]), e_iln, 16)
+
+    e_p, e_zero, e_p12 = ev(), ev(), ev()
+    inc(g.iota(T.pidx[:, 0:1], [[1, 1]], 0, 1), e_p)
+    inc(g.iota(T.gio[:, :], [[1, 4], [16, 8]], 0, 0), e_p)
+    e_vals = do(g.iota(T.vals[:, :], [[3 * NODES, 4], [3, NODES]], 2, 0))
+    inc(V.memset(T.d0[:, 0:4 * TR:3], 0.0), e_zero)
+    need("v", e_p)
+    inc(V.tensor_scalar(T.p12[:, 0:1], T.pidx[:, 0:1], 12, None, A.bitwise_and), e_p12)
+    inc(V.tensor_scalar(T.p3[:, 0:1], T.pidx[:, 0:1], 3, None, A.bitwise_and), e_p12)
+    inc(V.memset(T.d1[:, 2:4 * TR:3], 0.0), e_zero)
+    need("v", e_p12)
+    e_p12f = do(V.tensor_copy(T.p12f[:, 0:1], T.p12[:, 0:1]))
+    for b in (0, 1):
+        inc(V.memset(T.d1[:, TR * b + 1:TR * b + TR // 2:3], 0.0), e_zero)
+    need("v", e_p12f)
+    e_ppf = do(V.tensor_scalar(T.ppf[:, 0:1], T.p3[:, 0:1], 128.0, T.p12f[:, 0:1], A.mult, A.add))
+    for b in (2, 3):
+        inc(V.memset(T.d1[:, TR * b + 1:TR * b + TR // 2:3], 0.0), e_zero)
+    need("v", e_ppf)
+    e_glo = do(V.tensor_scalar(T.glo[:, :], T.gio[:, :], T.ppf[:, 0:1], None, A.add))
+    inc(V.memset(T.uu[:, 0:4 * UW:UW], 0.0), e_zero)
+    inc(V.memset(T.mk[:, :], 0.0), e_zero)
+
+    need("v", e_sn)
+    e_so = [ev(), ev(), ev()]
+    e_so.append(e_so[2])
+    for t in range(4):
+        inc(V.tensor_scalar(T["so%d" % t][:, :], T.snl[:, :], 4.0, float(t), A.mult, A.add), e_so[t])
+
+    def copy(q, out, src, e):
+        return inc(S.activation(out, src, Act.Copy) if q == "a" else V.tensor_copy(out, src), e)
+
+    def pick(q, t, at, e):
+        lo, hi = CAP * at[0], CAP * (at[-1] + 1)
+        copy(q, T.xg[:, 4 * lo + t:4 * hi:4], T.xt[:, 0:512].indirect(T["so%d" % t][:, lo // 16:hi // 16]), e)
+
+    def pack(dst, src, at):
+        a, b = CAP * at[0], CAP * (at[-1] + 1)
+        return do(V.quantize_mx(T[dst + "c"][:, a:b], T[dst + "p"][:, a:b], T[src][:, 4 * a:4 * b]))
+
+    need("a", e_x)
+    need("v", e_x)
+    for stage, at in enumerate(STAGES):
+        e_g = ev()
+        for t in (0, 1):
+            need("a", e_so[t])
+            pick("a", t, at, e_g)
+        for t in (2, 3):
+            need("v", e_so[t])
+            pick("v", t, at, e_g)
+        need("v", e_g)
+        need("g", pack("sx", "xg", at))
+        send("sx", "lx", stage, T.sem["ax%d" % stage], T.sem.sentx)
+
+    e_xo = ev()
+    for t in range(4):
+        need("a", e_so[t])
+        pick("a", t, (r,), e_xo)
+    need("a", e_gr, e_glo)
+    e_grp = ev()
+    for b in range(4):
+        copy("a", T.d1[:, TR * b:TR * b + TR // 2:3], T.grt[:, 0:512].indirect(T.glo[:, 8 * b:8 * b + 8]), e_grp)
+    need("v", e_nb)
+    e_4 = do(V.tensor_scalar(T.nb4[:, :], T.nbl[:, :], 4, None, A.arith_shift_right))
+    e_nbo = do(V.tensor_copy(T.nbo[:, :], T.nbl[:, :]))
+    e_56 = do(V.tensor_scalar(T.nb5[:, :], T.nbl[:, :], 40.0, None, A.mult))
+    need("v", e_4)
+    inc(V.tensor_scalar(T.nb6[:, :], T.nb4[:, :], -639.0, None, A.mult), e_56)
+    need("v", e_xo)
+    e_xoq = pack("lx", "xg", (r,))
+    need("v", e_56)
+    e = do(V.tensor_tensor(T.nb7[:, :], T.nb5[:, :], T.nb6[:, :], A.add))
+    need("v", e_w)
+    e_wq = do(V.quantize_mx(T.wqc[:, 0:512], T.wqp[:, 0:512], T.wt[:, 0:2048]))
+    need("v", e)
+    e = do(V.tensor_copy(T.nbi[:, :], T.nb7[:, :]))
+    need("v", e_zero)
+    e_mk = do(V.memset(T.mk[:, 2:TR:3], -1.0))
+    need("v", e, e_vals, e_inv)
+    e_sc = do(V.tensor_copy(T.inv[:, 0:SL].indirect(T.nbi[:, 0:32]), T.vals[:, 0:512]))
+    need("v", e_grp)
+    e_d1 = {}
+    for b in range(4):
+        e_d1[b] = ev()
+        src = T.d1[:, TR * b:TR * b + TR // 2:3]
+        inc(V.tensor_copy(T.d1[:, TR * b + TR // 2 + 1:TR * b + TR:3], src), e_d1[b])
+        inc(V.tensor_scalar(T.d1[:, TR * b + TR // 2:TR * b + TR:3], src, -1.0, None, A.mult), e_d1[b])
+    e_iv = ev()
+    need("s", e_sc)
+    for p in range(8):
+        inc(Y.dma_start(T.iv[16 * p:16 * p + 16, :], T.inv[0:1, :]), e_iv, 16)
+
+    e_dil, e_il, e_w2 = ev(), ev(), ev()
+    g.wait_ge(T.sem.sentx, sent)
+    for q in range(8):
+        inc(g.dma_start(T.dil[2 * q:2 * q + 2, :], T.il[:, q:64:8], allow_slow_non_contiguous=True), e_dil, 16)
+
+    last = {}
+
+    def products(st, mv, order, arrived):
+        out, met = {}, []
+        for b, late in order:
+            bank, a = (4 + b, FAR) if late else (b, NEAR)
+            if late and not met:
+                met.append(TE.wait_ge(arrived, arrive[1]))
+            if bank in last:
+                need("t", last[bank])
+            out[b, late] = do(TE.matmul_mx(T.ps[:, 512 * bank:512 * bank + HF], T[st + "c"][:, 128 * b:128 * b + 128], T[st + "p"][:, 128 * b:128 * b + 128],
+                                           T[mv + "c"][:, a:a + HF], T[mv + "p"][:, a:a + HF], True, True))
+        return out
+
+    def take(q, b, late, out, e_mm):
+        bank = 4 + b if late else b
+        need(q, e_mm[b, late])
+        last[bank] = copy(q, out, T.ps[:, 512 * bank:512 * bank + HF], ev())
+        return last[bank]
+
+    def zpart(b, late):
+        a = FAR if late else NEAR
+        return T["z%d" % b][:, a:a + HF]
+
+    def upart(b, late):
+        a = UW * b + 1 + (FAR if late else NEAR)
+        return T.uu[:, a:a + HF]
+
+    FIRST = ((0, 0), (1, 0), (0, 1), (1, 1), (2, 0), (2, 1), (3, 0), (3, 1))
+    need("t", e_wq, e_xoq)
+    TE.wait_ge(T.sem.ax0, arrive[0])
+    e_m = products("wq", "lx", FIRST, T.sem.ax1)
+    need("s", e_m[0, 1])
+    inc(Y.dma_start(T.w2t[:, :], T.w2[:, :]), e_w2, 16)
+    need("s", e_dil)
+    for p in range(8):
+        inc(Y.dma_start(T.ill[16 * p:16 * p + 16, :], T.dil[:, :]), e_il, 16)
+
+    e_z = {b: [] for b in range(4)}
+    e_zs, e_cc, e_mm, e_c, e_cp, e_ch, e_df = {}, {}, {}, {}, {}, {}, {}
+
+    def zs(b):
+        need("a", e_nbo, *e_z[b])
+        e_zs[b] = do(S.activation(T["zs%d" % b][:, :], T["z%d" % b][:, 0:SL].indirect(T.nbo[:, 16:32]), Act.Copy))
+
+    def pairs(b, out, op):
+        need("v", e_nbo, e_zs[b], *e_z[b])
+        return do(V.tensor_tensor(out, T["z%d" % b][:, 0:SL].indirect(T.nbo[:, 0:16]), T["zs%d" % b][:, :], op))
+
+    def cc(b):
+        e_cc[b] = pairs(b, T.d0[:, TR * b + 2:TR * b + TR:3], A.is_ge)
+
+    def mm(b):
+        e_mm[b] = pairs(b, T["mm%d" % b][:, :], A.max)
+
+    def c(b):
+        need("v", e_mm[b])
+        e_c[b] = do(V.tensor_tensor(T.d0[:, TR * b + 1:TR * b + TR // 2:3], T["mm%d" % b][:, 0:128], T["mm%d" % b][:, 128:256], A.is_ge))
+
+    def cp(b):
+        need("v", e_c[b])
+        e_cp[b] = do(V.tensor_copy(T.d0[:, TR * b + TR // 2 + 1:TR * b + TR:3], T.d0[:, TR * b + 1:TR * b + TR // 2:3]))
+
+    def ch(b):
+        need("v", e_zero, e_d1[b], e_cc[b], e_cp[b])
+        e_ch[b] = do(V.tensor_tensor_scan(T.gb[:, 2 * TR * b:2 * TR * b + TR], T.d0[:, TR * b:TR * b + TR], T.d1[:, TR * b:TR * b + TR], 0.0, A.mult, A.add))
+
+    def df(b):
+        need("v", e_mk, e_ch[b])
+        e_df[b] = do(V.tensor_tensor_scan(T.gb[:, 2 * TR * b + TR:2 * TR * b + 2 * TR], T.mk[:, :], T.gb[:, 2 * TR * b:2 * TR * b + TR], 0.0, A.mult, A.subtract))
+
+    def grad(q, b, lo, hi, e):
+        need(q, e_lt, e_ch[b], e_df[b])
+        copy(q, T.gt[:, 4 * lo + b:4 * hi:4], T.gb[:, 2 * TR * b:2 * TR * b + 2 * TR].indirect(T.lt[:, lo // 16:hi // 16]), e)
+
+    for b, late in FIRST:
+        e_z[b].append(take("a", b, late, zpart(b, late), e_m))
+        if late:
+            zs(b)
+    cc(0)
+    mm(0)
+    cc(1)
+    c(0)
+    mm(1)
+    cp(0)
+    c(1)
+    ch(0)
+    cp(1)
+    need("v", e_iv)
+    e_lt = do(V.tensor_copy(T.lt[:, :], T.iv[:, :]))
+    df(0)
+    cc(2)
+    ch(1)
+    mm(2)
+    df(1)
+    cc(3)
+    c(2)
+    mm(3)
+    cp(2)
+    c(3)
+    ch(2)
+    cp(3)
+    df(2)
+    ch(3)
+    df(3)
+    e_g0, e_g1, e_g2 = ev(), ev(), ev()
+    grad("a", 0, 0, SL, e_g0)
+    grad("a", 1, 0, SL, e_g0)
+    grad("a", 2, PART, PART + CAP, e_g0)
+    grad("a", 2, FAR, FAR + HF, e_g1)
+    grad("a", 3, FAR, FAR + HF, e_g1)
+    grad("v", 3, PART, PART + CAP, e_g0)
+    need("v", e_g0)
+    need("g", pack("sg", "gt", STAGES[0]))
+    send("sg", "lg", 0, T.sem.ag0, T.sem.sentg)
+    need("v", e_g1)
+    need("g", pack("sg", "gt", STAGES[1]))
+    send("sg", "lg", 1, T.sem.ag1, T.sem.sentg)
+
+    for b in (2, 3):
+        grad("a", b, OWN, OWN + CAP, e_g2)
+    e = do(V.memset(T.rs[:, :], 1.0))
+    need("v", e_w2)
+    e_vq = do(V.quantize_mx(T.vqc[:, 0:512], T.vqp[:, 0:512], T.w2t[:, 0:2048]))
+    need("v", e_g2)
+    e_goq = pack("lg", "gt", (r,))
+    need("v", e)
+    e_rs = do(V.memset(T.rs[:, 0:F * NODES:F], 0.0))
+    need("v", e_il, e_iln)
+    e_ilo = do(V.tensor_scalar(T.ilo[:, :], T.ill[:, :], 1.0, None, A.add))
+    e_ilp = do(V.tensor_scalar(T.ilp[:, :], T.iln[:, :], 1.0, None, A.add))
+
+    need("t", e_vq, e_goq)
+    TE.wait_ge(T.sem.ag0, arrive[0])
+    e_m = products("vq", "lg", ((0, 0), (2, 0), (1, 0), (0, 1), (2, 1), (1, 1), (3, 0), (3, 1)), T.sem.ag1)
+
+    e_u = {b: [] for b in range(4)}
+    e_ac, e_ug, e_us, e_y = {}, {}, {}, ev()
+
+    def win(b):
+        return T.uu[:, UW * b:UW * b + SL + 1]
+
+    def bring(q, b, late):
+        e_u[b].append(take(q, b, late, upart(b, late), e_m))
+
+    def places(b):
+        need("a", e_ilo, e_zero, *e_u[b])
+        e_ac[b] = do(S.activation(T["ac%d0" % b][:, :], win(b).indirect(T.ilo[:, 48:64]), Act.Copy))
+
+    def every(b):
+        need("a", e_ilp, e_zero, *e_u[b])
+        e_ug[b] = do(S.activation(T["ug%d" % b][:, :], win(b).indirect(T.ilp[:, 0:64]), Act.Copy))
+
+    def add(b, i):
+        need("v", e_ilo, e_ac[b], *e_u[b])
+        e_ac[b] = do(V.tensor_tensor(T["ac%d%d" % (b, i + 1)][:, :], win(b).indirect(T.ilo[:, 16 * i:16 * i + 16]), T["ac%d%d" % (b, i)][:, :], A.add))
+
+    def scan(b):
+        need("v", e_rs, e_ug[b])
+        e_us[b] = do(V.tensor_tensor_scan(T["us%d" % b][:, :], T.rs[:, :], T["ug%d" % b][:, :], 0.0, A.mult, A.add))
+
+    def out(q, b):
+        e = ev()
+        if b % 2:
+            need(q, e_us[b])
+            copy(q, T["yo%d" % b][:, :], T["us%d" % b][:, F - 1:F * NODES:F], e)
+        else:
+            need(q, e_ac[b])
+            inc(V.tensor_tensor(T["yo%d" % b][:, :], T["ac%d3" % b][:, 0:128], T["ac%d3" % b][:, 128:256], A.add), e)
+        need("s", e)
+        inc(Y.dma_start(T.y[:, 128 * b:128 * b + 128], T["yo%d" % b][:, :]), e_y, 16)
+
+    bring("a", 0, 0)
+    bring("v", 2, 0)
+    bring("v", 1, 0)
+    bring("a", 0, 1)
+    bring("v", 2, 1)
+    places(0)
+    bring("v", 1, 1)
+    places(2)
+    every(1)
+    bring("a", 3, 0)
+    bring("a", 3, 1)
+    every(3)
+    for i in range(3):
+        add(0, i)
+        add(2, i)
+    out("v", 0)
+    scan(1)
+    out("v", 2)
+    scan(3)
+    out("a", 1)
+    out("v", 3)
+    need("s", e_y)
+    g.wait_ge(T.sem.sentg, sent)
+    for e in made:
+        if not e["w"]:
+            need("g", e)

@@ -6,25 +6,25 @@ N, NODES, CAP, F = 4, 128, 160, 8
 SL = N * CAP
 HF = 2 * CAP
 UW = SL + 8
-TR = 3 * 2 * NODES
-ORDER = (0, 2, 1, 3)
+ST = 7
+TR = ST * NODES
 
 SCRATCH = {
     "snl": ("sbuf", [128, SL // 16], "int32"), "nbl": ("sbuf", [128, 32], "int32"), "dnb": ("dram", [16, 32], "int32"),
     "nbo": ("sbuf", [128, 32], "uint16"), "nbi": ("sbuf", [128, 32], "uint16"),
-    "ill": ("sbuf", [128, 64], "int32"), "ilo": ("sbuf", [128, 64], "uint16"), "dil": ("dram", [16, 64], "int32"),
-    "iln": ("sbuf", [128, 64], "int32"), "ilp": ("sbuf", [128, 64], "uint16"),
+    "ill": ("sbuf", [128, 128], "int32"), "ilo": ("sbuf", [128, 128], "uint16"), "dil": ("dram", [16, 128], "int32"),
     "glo": ("sbuf", [128, 32], "uint16"), "gio": ("sbuf", [128, 32], "int32"),
-    "pidx": ("sbuf", [128, 1], "int32"), "p12": ("sbuf", [128, 1], "int32"), "p3": ("sbuf", [128, 1], "int32"),
-    "p12f": ("sbuf", [128, 1], "float32"), "ppf": ("sbuf", [128, 1], "float32"),
+    "pidx": ("sbuf", [128, 1], "int32"), "p12": ("sbuf", [128, 1], "int32"), "ppf": ("sbuf", [128, 1], "float32"),
+    "uio": ("sbuf", [128, 8], "int32"), "ui7": ("sbuf", [128, 8], "int32"), "uno": ("sbuf", [128, 8], "uint16"),
+    "yh0": ("sbuf", [128, 128], "float32"), "yh2": ("sbuf", [128, 128], "float32"),
     "vals": ("sbuf", [128, 512], "int32"), "inv": ("sbuf", [128, SL], "int32"),
     "iv": ("sbuf", [128, 40], "int32"), "lt": ("sbuf", [128, 40], "uint16"),
     "xt": ("sbuf", [128, 512], "bfloat16"), "grt": ("sbuf", [128, 512], "bfloat16"),
     "wt": ("sbuf", [128, 2048], "bfloat16"), "w2t": ("sbuf", [128, 2048], "bfloat16"),
     "xg": ("sbuf", [128, 4 * SL], "bfloat16"), "gt": ("sbuf", [128, 4 * SL], "bfloat16"),
     "d0": ("sbuf", [128, 4 * TR], "bfloat16"), "d1": ("sbuf", [128, 4 * TR], "bfloat16"),
-    "mk": ("sbuf", [128, TR], "bfloat16"), "gb": ("sbuf", [128, 8 * TR], "bfloat16"),
-    "rs": ("sbuf", [128, F * NODES], "float32"),
+    "gb": ("sbuf", [128, 4 * TR], "bfloat16"),
+    "rs": ("sbuf", [128, F * NODES], "bfloat16"),
     "uu": ("sbuf", [128, 4 * UW], "float32"),
     "ps": ("psum", [128, 4096], "float32"),
 }
@@ -36,8 +36,8 @@ for _n, _w in (("wq", 512), ("vq", 512), ("sx", SL), ("sg", SL), ("lx", SL), ("l
 for _b in range(4):
     SCRATCH["so%d" % _b] = ("sbuf", [128, SL // 16], "uint16")
     SCRATCH["z%d" % _b] = ("sbuf", [128, SL], "float32")
-    SCRATCH["zs%d" % _b] = ("sbuf", [128, 256], "float32")
-    SCRATCH["mm%d" % _b] = ("sbuf", [128, 256], "float32")
+    for _n in ("zs", "ma", "mb"):
+        SCRATCH["%s%d" % (_n, _b)] = ("sbuf", [128, NODES], "float32")
     if _b % 2:
         SCRATCH["ug%d" % _b] = ("sbuf", [128, F * NODES], "float32")
         SCRATCH["us%d" % _b] = ("sbuf", [128, F * NODES], "float32")
@@ -62,7 +62,7 @@ def rank_program(g, core, T, topo):
     pair = r - r % 2
     far = N // 2 - pair
     mate = pair + 1 - r % 2
-    STAGES = ((mate,), (far, far + 1))
+    MATE, FARS = (mate,), (far, far + 1)
     OWN, PART, NEAR, FAR = CAP * r, CAP * mate, CAP * pair, CAP * far
 
     made, seen = [], set()
@@ -87,10 +87,10 @@ def rank_program(g, core, T, topo):
                 e["w"] = True
                 Q[q].wait_ge(e["s"], e["n"])
 
-    def send(src, dst, stage, arrived, left):
+    def send(src, dst, to, arrived, left):
         for part in (0, 1):
             tr = []
-            for i, d in enumerate(STAGES[stage]):
+            for i, d in enumerate(to):
                 rid, pid, _ = topo.addr(cores[d])
                 es = topo.engines(cores[r], cores[d])[(part + i) % 2::2]
                 a, b = CAP * d, CAP * r
@@ -102,8 +102,10 @@ def rank_program(g, core, T, topo):
                                             remote_sem=arrived, src=f, dst=t))
             g.remote_dma_fused(tr, local_sem=left)
 
-    arrive = [sum(len(topo.engines(cores[s], cores[r])) for s in st) for st in STAGES]
-    sent = sum(len(topo.engines(cores[r], cores[d])) for st in STAGES for d in st)
+    def arrive(at):
+        return sum(len(topo.engines(cores[s], cores[r])) for s in at)
+
+    sent = sum(len(topo.engines(cores[r], cores[d])) for d in MATE + FARS)
 
     e_x, e_sn, e_w, e_dnb, e_nb, e_gr, e_inv, e_iln = ev(), ev(), ev(), ev(), ev(), ev(), ev(), ev()
     inc(Y.dma_start(T.xt[:, :], T.x[:, :]), e_x, 16)
@@ -111,43 +113,38 @@ def rank_program(g, core, T, topo):
         inc(Y.dma_start(T.snl[16 * p:16 * p + 16, :], T.sn[:, :]), e_sn, 16)
     for p in range(4, 8):
         inc(S.dma_start(T.snl[16 * p:16 * p + 16, :], T.sn[:, :]), e_sn, 16)
-    for i, k in enumerate(ORDER):
-        inc(S.dma_start(T.dnb[:, 8 * i:8 * i + 8], T.nb[k:16:4, :]), e_dnb, 16)
+    for k in range(4):
+        inc(S.dma_start(T.dnb[:, 8 * k:8 * k + 8], T.nb[k:16:4, :]), e_dnb, 16)
     inc(S.dma_start(T.wt[:, :], T.w[:, :]), e_w, 16)
     inc(Y.dma_start(T.grt[:, :], T.gr[:, :]), e_gr, 16)
     inc(Y.dma_start(T.inv[0:1, :], T.sn[:, :]), e_inv, 16)
     need("s", e_dnb)
     for p in range(8):
         inc(Y.dma_start(T.nbl[16 * p:16 * p + 16, :], T.dnb[:, :]), e_nb, 16)
-    for p in range(8):
-        inc(Y.dma_start(T.iln[16 * p:16 * p + 16, :], T.il[:, :]), e_iln, 16)
+    e_dil, e_w2 = ev(), ev()
 
-    e_p, e_zero, e_p12 = ev(), ev(), ev()
-    inc(g.iota(T.pidx[:, 0:1], [[1, 1]], 0, 1), e_p)
+    e_p, e_zero, e_p12, e_vals = ev(), ev(), ev(), ev()
+    inc(g.iota(T.pidx[:, 0:1], [[1, 1]], 0, 129), e_p)
     inc(g.iota(T.gio[:, :], [[1, 4], [16, 8]], 0, 0), e_p)
-    e_vals = do(g.iota(T.vals[:, :], [[3 * NODES, 4], [3, NODES]], 2, 0))
-    inc(V.memset(T.d0[:, 0:4 * TR:3], 0.0), e_zero)
+    inc(g.iota(T.uio[:, :], [[1, 8]], 0, 8), e_p)
+    inc(g.iota(T.vals[:, 0:2 * NODES], [[2, 2], [ST, NODES]], 4, 0), e_vals)
+    inc(g.iota(T.vals[:, 2 * NODES:4 * NODES], [[-1, 2], [ST, NODES]], 2, 0), e_vals)
+    inc(V.memset(T.d1[:, 0:4 * TR:ST], 0.0), e_zero)
+    inc(V.memset(T.d0[:, 0:4 * TR:ST], 0.0), e_zero)
     need("v", e_p)
-    inc(V.tensor_scalar(T.p12[:, 0:1], T.pidx[:, 0:1], 12, None, A.bitwise_and), e_p12)
-    inc(V.tensor_scalar(T.p3[:, 0:1], T.pidx[:, 0:1], 3, None, A.bitwise_and), e_p12)
-    inc(V.memset(T.d1[:, 2:4 * TR:3], 0.0), e_zero)
+    inc(V.tensor_scalar(T.p12[:, 0:1], T.pidx[:, 0:1], 3 * 128 + 12, None, A.bitwise_and), e_p12)
+    inc(V.tensor_scalar(T.ui7[:, :], T.uio[:, :], 127, None, A.bitwise_and), e_p12)
+    inc(V.memset(T.d0[:, 4:4 * TR:ST], 0.0), e_zero)
     need("v", e_p12)
-    e_p12f = do(V.tensor_copy(T.p12f[:, 0:1], T.p12[:, 0:1]))
-    for b in (0, 1):
-        inc(V.memset(T.d1[:, TR * b + 1:TR * b + TR // 2:3], 0.0), e_zero)
-    need("v", e_p12f)
-    e_ppf = do(V.tensor_scalar(T.ppf[:, 0:1], T.p3[:, 0:1], 128.0, T.p12f[:, 0:1], A.mult, A.add))
-    for b in (2, 3):
-        inc(V.memset(T.d1[:, TR * b + 1:TR * b + TR // 2:3], 0.0), e_zero)
+    e_ppf = do(V.tensor_copy(T.ppf[:, 0:1], T.p12[:, 0:1]))
+    e_uno = do(V.tensor_copy(T.uno[:, :], T.ui7[:, :]))
+    inc(V.memset(T.d0[:, 6:4 * TR:ST], 0.0), e_zero)
     need("v", e_ppf)
     e_glo = do(V.tensor_scalar(T.glo[:, :], T.gio[:, :], T.ppf[:, 0:1], None, A.add))
-    inc(V.memset(T.uu[:, 0:4 * UW:UW], 0.0), e_zero)
-    inc(V.memset(T.mk[:, :], 0.0), e_zero)
 
     need("v", e_sn)
-    e_so = [ev(), ev(), ev()]
-    e_so.append(e_so[2])
-    for t in range(4):
+    e_so = [ev(), ev(), ev(), ev()]
+    for t in (0, 2, 1, 3):
         inc(V.tensor_scalar(T["so%d" % t][:, :], T.snl[:, :], 4.0, float(t), A.mult, A.add), e_so[t])
 
     def copy(q, out, src, e):
@@ -163,7 +160,7 @@ def rank_program(g, core, T, topo):
 
     need("a", e_x)
     need("v", e_x)
-    for stage, at in enumerate(STAGES):
+    for stage, at in enumerate((MATE, FARS)):
         e_g = ev()
         for t in (0, 1):
             need("a", e_so[t])
@@ -173,203 +170,199 @@ def rank_program(g, core, T, topo):
             pick("v", t, at, e_g)
         need("v", e_g)
         need("g", pack("sx", "xg", at))
-        send("sx", "lx", stage, T.sem["ax%d" % stage], T.sem.sentx)
+        send("sx", "lx", at, T.sem["ax%d" % stage], T.sem.sentx)
 
     e_xo = ev()
     for t in range(4):
         need("a", e_so[t])
         pick("a", t, (r,), e_xo)
+    e_ch = {}
     need("a", e_gr, e_glo)
-    e_grp = ev()
-    for b in range(4):
-        copy("a", T.d1[:, TR * b:TR * b + TR // 2:3], T.grt[:, 0:512].indirect(T.glo[:, 8 * b:8 * b + 8]), e_grp)
+    e_gp1 = copy("a", T.d0[:, 1:4 * TR:ST], T.grt[:, 0:512].indirect(T.glo[:, 0:32]), ev())
     need("v", e_nb)
     e_4 = do(V.tensor_scalar(T.nb4[:, :], T.nbl[:, :], 4, None, A.arith_shift_right))
     e_nbo = do(V.tensor_copy(T.nbo[:, :], T.nbl[:, :]))
     e_56 = do(V.tensor_scalar(T.nb5[:, :], T.nbl[:, :], 40.0, None, A.mult))
     need("v", e_4)
     inc(V.tensor_scalar(T.nb6[:, :], T.nb4[:, :], -639.0, None, A.mult), e_56)
-    need("v", e_xo)
-    e_xoq = pack("lx", "xg", (r,))
-    need("v", e_56)
-    e = do(V.tensor_tensor(T.nb7[:, :], T.nb5[:, :], T.nb6[:, :], A.add))
     need("v", e_w)
     e_wq = do(V.quantize_mx(T.wqc[:, 0:512], T.wqp[:, 0:512], T.wt[:, 0:2048]))
+    need("v", e_56)
+    e = do(V.tensor_tensor(T.nb7[:, :], T.nb5[:, :], T.nb6[:, :], A.add))
+    need("v", e_xo)
+    e_xoq = pack("lx", "xg", (r,))
     need("v", e)
     e = do(V.tensor_copy(T.nbi[:, :], T.nb7[:, :]))
-    need("v", e_zero)
-    e_mk = do(V.memset(T.mk[:, 2:TR:3], -1.0))
+    e_d0 = ev()
+    need("g", e_gp1)
+    for step in (2, 3, 5):
+        inc(g.affine_select(T.d0[:, step:4 * TR:ST], T.d0[:, 1:4 * TR:ST], [[0, 4 * NODES]], A.is_ge, 0.0, 0, 0), e_d0)
+    e_one = do(g.iota(T.rs[:, :], [[0, F * NODES]], 1, 0, allow_small_or_imprecise_dtypes=True))
+    need("g", e_one)
+    e_rs = do(g.iota(T.rs[:, 0:F * NODES:F], [[0, NODES]], 0, 0, allow_small_or_imprecise_dtypes=True))
+    e_uz = do(V.memset(T.uu[:, 0:4 * UW:UW], 0.0))
     need("v", e, e_vals, e_inv)
     e_sc = do(V.tensor_copy(T.inv[:, 0:SL].indirect(T.nbi[:, 0:32]), T.vals[:, 0:512]))
-    need("v", e_grp)
-    e_d1 = {}
-    for b in range(4):
-        e_d1[b] = ev()
-        src = T.d1[:, TR * b:TR * b + TR // 2:3]
-        inc(V.tensor_copy(T.d1[:, TR * b + TR // 2 + 1:TR * b + TR:3], src), e_d1[b])
-        inc(V.tensor_scalar(T.d1[:, TR * b + TR // 2:TR * b + TR:3], src, -1.0, None, A.mult), e_d1[b])
     e_iv = ev()
     need("s", e_sc)
     for p in range(8):
         inc(Y.dma_start(T.iv[16 * p:16 * p + 16, :], T.inv[0:1, :]), e_iv, 16)
 
-    e_dil, e_il, e_w2 = ev(), ev(), ev()
     g.wait_ge(T.sem.sentx, sent)
-    for q in range(8):
-        inc(g.dma_start(T.dil[2 * q:2 * q + 2, :], T.il[:, q:64:8], allow_slow_non_contiguous=True), e_dil, 16)
 
     last = {}
 
-    def products(st, mv, order, arrived):
-        out, met = {}, []
-        for b, late in order:
-            bank, a = (4 + b, FAR) if late else (b, NEAR)
-            if late and not met:
-                met.append(TE.wait_ge(arrived, arrive[1]))
-            if bank in last:
-                need("t", last[bank])
-            out[b, late] = do(TE.matmul_mx(T.ps[:, 512 * bank:512 * bank + HF], T[st + "c"][:, 128 * b:128 * b + 128], T[st + "p"][:, 128 * b:128 * b + 128],
-                                           T[mv + "c"][:, a:a + HF], T[mv + "p"][:, a:a + HF], True, True))
-        return out
+    def product(st, mv, b, bank, a, n):
+        if bank in last:
+            need("t", last[bank])
+        return do(TE.matmul_mx(T.ps[:, 512 * bank:512 * bank + n], T[st + "c"][:, 128 * b:128 * b + 128], T[st + "p"][:, 128 * b:128 * b + 128],
+                               T[mv + "c"][:, a:a + n], T[mv + "p"][:, a:a + n], True, True))
 
-    def take(q, b, late, out, e_mm):
-        bank = 4 + b if late else b
-        need(q, e_mm[b, late])
-        last[bank] = copy(q, out, T.ps[:, 512 * bank:512 * bank + HF], ev())
+    def take(q, bank, out, n, e_mm):
+        need(q, e_mm)
+        last[bank] = copy(q, out, T.ps[:, 512 * bank:512 * bank + n], ev())
         return last[bank]
-
-    def zpart(b, late):
-        a = FAR if late else NEAR
-        return T["z%d" % b][:, a:a + HF]
-
-    def upart(b, late):
-        a = UW * b + 1 + (FAR if late else NEAR)
-        return T.uu[:, a:a + HF]
 
     FIRST = ((0, 0), (1, 0), (0, 1), (1, 1), (2, 0), (2, 1), (3, 0), (3, 1))
     need("t", e_wq, e_xoq)
-    TE.wait_ge(T.sem.ax0, arrive[0])
-    e_m = products("wq", "lx", FIRST, T.sem.ax1)
+    TE.wait_ge(T.sem.ax0, arrive(MATE))
+    e_m = {}
+    for b, late in FIRST:
+        if (b, late) == (0, 1):
+            TE.wait_ge(T.sem.ax1, arrive(FARS))
+        e_m[b, late] = product("wq", "lx", b, b + 4 * late, FAR if late else NEAR, HF)
     need("s", e_m[0, 1])
     inc(Y.dma_start(T.w2t[:, :], T.w2[:, :]), e_w2, 16)
+    for f in range(F):
+        inc(Y.dma_start(T.dil[:, 8 * f:8 * f + 8], T.il[f:16:F, :]), e_dil, 16)
+    inc(Y.dma_start(T.dil[:, 64:128], T.il[:, :]), e_dil, 16)
     need("s", e_dil)
     for p in range(8):
-        inc(Y.dma_start(T.ill[16 * p:16 * p + 16, :], T.dil[:, :]), e_il, 16)
+        inc(Y.dma_start(T.ill[16 * p:16 * p + 16, :], T.dil[:, :]), e_iln, 16)
 
     e_z = {b: [] for b in range(4)}
-    e_zs, e_cc, e_mm, e_c, e_cp, e_ch, e_df = {}, {}, {}, {}, {}, {}, {}
+    e_zs, e_ma, e_mb, e_k = {}, {}, {}, {b: ev() for b in range(4)}
+
+    def nbr(b, k):
+        return T["z%d" % b][:, 0:SL].indirect(T.nbo[:, 8 * k:8 * k + 8])
+
+    def zcopy(b, late):
+        a = FAR if late else NEAR
+        e_z[b].append(take("a", b + 4 * late, T["z%d" % b][:, a:a + HF], HF, e_m[b, late]))
 
     def zs(b):
         need("a", e_nbo, *e_z[b])
-        e_zs[b] = do(S.activation(T["zs%d" % b][:, :], T["z%d" % b][:, 0:SL].indirect(T.nbo[:, 16:32]), Act.Copy))
+        e_zs[b] = do(S.activation(T["zs%d" % b][:, :], nbr(b, 1), Act.Copy))
 
-    def pairs(b, out, op):
+    def mask(b, step):
+        return T.d1[:, TR * b + step:TR * b + TR:ST]
+
+    def m01(b):
         need("v", e_nbo, e_zs[b], *e_z[b])
-        return do(V.tensor_tensor(out, T["z%d" % b][:, 0:SL].indirect(T.nbo[:, 0:16]), T["zs%d" % b][:, :], op))
+        e_ma[b] = do(V.tensor_tensor(T["ma%d" % b][:, :], nbr(b, 0), T["zs%d" % b][:, :], A.max))
 
-    def cc(b):
-        e_cc[b] = pairs(b, T.d0[:, TR * b + 2:TR * b + TR:3], A.is_ge)
+    def q0(b):
+        inc(V.tensor_tensor(mask(b, 4), nbr(b, 0), T["zs%d" % b][:, :], A.is_ge), e_k[b])
 
-    def mm(b):
-        e_mm[b] = pairs(b, T["mm%d" % b][:, :], A.max)
+    def m012(b):
+        need("v", e_ma[b])
+        e_mb[b] = do(V.tensor_tensor(T["mb%d" % b][:, :], nbr(b, 2), T["ma%d" % b][:, :], A.max))
 
-    def c(b):
-        need("v", e_mm[b])
-        e_c[b] = do(V.tensor_tensor(T.d0[:, TR * b + 1:TR * b + TR // 2:3], T["mm%d" % b][:, 0:128], T["mm%d" % b][:, 128:256], A.is_ge))
+    def p2(b):
+        need("v", e_ma[b])
+        e_p2[b] = do(V.tensor_tensor(mask(b, 2), nbr(b, 2), T["ma%d" % b][:, :], A.is_gt))
 
-    def cp(b):
-        need("v", e_c[b])
-        e_cp[b] = do(V.tensor_copy(T.d0[:, TR * b + TR // 2 + 1:TR * b + TR:3], T.d0[:, TR * b + 1:TR * b + TR // 2:3]))
+    def w3(b):
+        need("v", e_mb[b])
+        e_w3[b] = do(V.tensor_tensor(mask(b, 1), nbr(b, 3), T["mb%d" % b][:, :], A.is_gt))
+
+    def n2(b):
+        need("v", e_p2[b])
+        inc(V.tensor_scalar(mask(b, 6), mask(b, 2), -1.0, 1.0, A.mult, A.add), e_k[b])
+
+    def n3(b):
+        need("v", e_w3[b])
+        for step in (3, 5):
+            inc(V.tensor_scalar(mask(b, step), mask(b, 1), -1.0, None, A.add), e_k[b])
 
     def ch(b):
-        need("v", e_zero, e_d1[b], e_cc[b], e_cp[b])
-        e_ch[b] = do(V.tensor_tensor_scan(T.gb[:, 2 * TR * b:2 * TR * b + TR], T.d0[:, TR * b:TR * b + TR], T.d1[:, TR * b:TR * b + TR], 0.0, A.mult, A.add))
-
-    def df(b):
-        need("v", e_mk, e_ch[b])
-        e_df[b] = do(V.tensor_tensor_scan(T.gb[:, 2 * TR * b + TR:2 * TR * b + 2 * TR], T.mk[:, :], T.gb[:, 2 * TR * b:2 * TR * b + TR], 0.0, A.mult, A.subtract))
+        need("v", e_zero, e_d0, e_k[b])
+        e_ch[b] = do(V.tensor_tensor_scan(T.gb[:, TR * b:TR * b + TR], T.d0[:, TR * b:TR * b + TR], T.d1[:, TR * b:TR * b + TR], 0.0, A.subtract, A.mult))
 
     def grad(q, b, lo, hi, e):
-        need(q, e_lt, e_ch[b], e_df[b])
-        copy(q, T.gt[:, 4 * lo + b:4 * hi:4], T.gb[:, 2 * TR * b:2 * TR * b + 2 * TR].indirect(T.lt[:, lo // 16:hi // 16]), e)
+        need(q, e_lt, e_ch[b])
+        copy(q, T.gt[:, 4 * lo + b:4 * hi:4], T.gb[:, TR * b:TR * b + TR].indirect(T.lt[:, lo // 16:hi // 16]), e)
 
     for b, late in FIRST:
-        e_z[b].append(take("a", b, late, zpart(b, late), e_m))
+        zcopy(b, late)
         if late:
             zs(b)
-    cc(0)
-    mm(0)
-    cc(1)
-    c(0)
-    mm(1)
-    cp(0)
-    c(1)
-    ch(0)
-    cp(1)
-    need("v", e_iv)
-    e_lt = do(V.tensor_copy(T.lt[:, :], T.iv[:, :]))
-    df(0)
-    cc(2)
-    ch(1)
-    mm(2)
-    df(1)
-    cc(3)
-    c(2)
-    mm(3)
-    cp(2)
-    c(3)
-    ch(2)
-    cp(3)
-    df(2)
-    ch(3)
-    df(3)
-    e_g0, e_g1, e_g2 = ev(), ev(), ev()
-    grad("a", 0, 0, SL, e_g0)
-    grad("a", 1, 0, SL, e_g0)
-    grad("a", 2, PART, PART + CAP, e_g0)
-    grad("a", 2, FAR, FAR + HF, e_g1)
-    grad("a", 3, FAR, FAR + HF, e_g1)
-    grad("v", 3, PART, PART + CAP, e_g0)
-    need("v", e_g0)
-    need("g", pack("sg", "gt", STAGES[0]))
-    send("sg", "lg", 0, T.sem.ag0, T.sem.sentg)
-    need("v", e_g1)
-    need("g", pack("sg", "gt", STAGES[1]))
-    send("sg", "lg", 1, T.sem.ag1, T.sem.sentg)
+    e_gf, e_gp, e_go, e_gf0, e_p2, e_w3 = ev(), ev(), ev(), ev(), {}, {}
+    for b in range(4):
+        if b == 0:
+            m01(b)
+            q0(b)
+            m012(b)
+        p2(b)
+        w3(b)
+        if b == 3:
+            q0(b)
+        n2(b)
+        if b < 3:
+            m01(b + 1)
+        n3(b)
+        if b < 2:
+            q0(b + 1)
+        if b < 3:
+            m012(b + 1)
+        ch(b)
+        if b == 0:
+            need("v", e_iv)
+            e_lt = do(V.tensor_copy(T.lt[:, :], T.iv[:, :]))
+        if b < 2:
+            grad("a", b, 0, SL, e_gf0)
+    grad("a", 2, PART, PART + CAP, e_gp)
+    grad("a", 2, FAR, FAR + HF, e_gf)
+    grad("v", 3, PART, PART + CAP, e_gp)
+    grad("a", 3, FAR, FAR + HF, e_gf)
+    need("v", e_gf0, e_gp)
+    need("g", pack("sg", "gt", MATE))
+    send("sg", "lg", MATE, T.sem.ag1, T.sem.sentg)
+    need("v", e_gf)
+    need("g", pack("sg", "gt", FARS))
+    send("sg", "lg", FARS, T.sem.ag0, T.sem.sentg)
 
     for b in (2, 3):
-        grad("a", b, OWN, OWN + CAP, e_g2)
-    e = do(V.memset(T.rs[:, :], 1.0))
+        grad("a", b, OWN, OWN + CAP, e_go)
     need("v", e_w2)
     e_vq = do(V.quantize_mx(T.vqc[:, 0:512], T.vqp[:, 0:512], T.w2t[:, 0:2048]))
-    need("v", e_g2)
+    need("v", e_go)
     e_goq = pack("lg", "gt", (r,))
-    need("v", e)
-    e_rs = do(V.memset(T.rs[:, 0:F * NODES:F], 0.0))
-    need("v", e_il, e_iln)
+    need("v", e_iln)
     e_ilo = do(V.tensor_scalar(T.ilo[:, :], T.ill[:, :], 1.0, None, A.add))
-    e_ilp = do(V.tensor_scalar(T.ilp[:, :], T.iln[:, :], 1.0, None, A.add))
 
-    need("t", e_vq, e_goq)
-    TE.wait_ge(T.sem.ag0, arrive[0])
-    e_m = products("vq", "lg", ((0, 0), (2, 0), (1, 0), (0, 1), (2, 1), (1, 1), (3, 0), (3, 1)), T.sem.ag1)
+    e_u = {b: [e_uz] for b in range(4)}
+    e_ac, e_ug, e_us, e_yh, e_y = {}, {}, {}, {}, ev()
+    RUN = {"o": (OWN, CAP, 0), "f": (FAR, HF, 4), "p": (PART, CAP, 0)}
 
-    e_u = {b: [] for b in range(4)}
-    e_ac, e_ug, e_us, e_y = {}, {}, {}, ev()
+    def mult(b, run):
+        a, n, bank = RUN[run]
+        e_m[b, run] = product("vq", "lg", b, bank + b, a, n)
 
     def win(b):
         return T.uu[:, UW * b:UW * b + SL + 1]
 
-    def bring(q, b, late):
-        e_u[b].append(take(q, b, late, upart(b, late), e_m))
+    def bring(q, b, run):
+        a, n, bank = RUN[run]
+        e_u[b].append(take(q, bank + b, T.uu[:, UW * b + 1 + a:UW * b + 1 + a + n], n, e_m[b, run]))
 
     def places(b):
-        need("a", e_ilo, e_zero, *e_u[b])
+        need("a", e_ilo, *e_u[b])
         e_ac[b] = do(S.activation(T["ac%d0" % b][:, :], win(b).indirect(T.ilo[:, 48:64]), Act.Copy))
 
     def every(b):
-        need("a", e_ilp, e_zero, *e_u[b])
-        e_ug[b] = do(S.activation(T["ug%d" % b][:, :], win(b).indirect(T.ilp[:, 0:64]), Act.Copy))
+        need("a", e_ilo, *e_u[b])
+        e_ug[b] = do(S.activation(T["ug%d" % b][:, :], win(b).indirect(T.ilo[:, 64:128]), Act.Copy))
 
     def add(b, i):
         need("v", e_ilo, e_ac[b], *e_u[b])
@@ -379,38 +372,57 @@ def rank_program(g, core, T, topo):
         need("v", e_rs, e_ug[b])
         e_us[b] = do(V.tensor_tensor_scan(T["us%d" % b][:, :], T.rs[:, :], T["ug%d" % b][:, :], 0.0, A.mult, A.add))
 
+    def half(q, b):
+        need(q, e_uno, e_ac[b])
+        e_yh[b] = copy(q, T["yh%d" % b][:, :], T["ac%d3" % b][:, 128:256].indirect(T.uno[:, :]), ev())
+
     def out(q, b):
         e = ev()
         if b % 2:
             need(q, e_us[b])
             copy(q, T["yo%d" % b][:, :], T["us%d" % b][:, F - 1:F * NODES:F], e)
         else:
-            need(q, e_ac[b])
-            inc(V.tensor_tensor(T["yo%d" % b][:, :], T["ac%d3" % b][:, 0:128], T["ac%d3" % b][:, 128:256], A.add), e)
+            need(q, e_ac[b], e_yh[b])
+            inc(V.tensor_tensor(T["yo%d" % b][:, :], T["ac%d3" % b][:, 0:128].indirect(T.uno[:, :]), T["yh%d" % b][:, :], A.add), e)
         need("s", e)
         inc(Y.dma_start(T.y[:, 128 * b:128 * b + 128], T["yo%d" % b][:, :]), e_y, 16)
 
-    bring("a", 0, 0)
-    bring("v", 2, 0)
-    bring("v", 1, 0)
-    bring("a", 0, 1)
-    bring("v", 2, 1)
+    need("t", e_vq, e_goq)
+    for b in (0, 2, 1, 3):
+        mult(b, "o")
+    bring("a", 0, "o")
+    bring("v", 2, "o")
+    bring("a", 1, "o")
+    bring("v", 3, "o")
+    TE.wait_ge(T.sem.ag1, arrive(MATE))
+    for b in (0, 2, 1, 3):
+        mult(b, "p")
+    TE.wait_ge(T.sem.ag0, arrive(FARS))
+    for b in (0, 2, 1, 3):
+        mult(b, "f")
+    bring("a", 0, "p")
+    bring("v", 2, "p")
+    bring("a", 1, "p")
+    bring("v", 3, "p")
+    bring("a", 0, "f")
+    bring("v", 2, "f")
     places(0)
-    bring("v", 1, 1)
+    bring("v", 1, "f")
+    bring("v", 3, "f")
     places(2)
     every(1)
-    bring("a", 3, 0)
-    bring("a", 3, 1)
     every(3)
     for i in range(3):
         add(0, i)
         add(2, i)
-    out("v", 0)
+    half("a", 0)
+    half("a", 2)
     scan(1)
-    out("v", 2)
     scan(3)
     out("a", 1)
-    out("v", 3)
+    out("v", 0)
+    out("v", 2)
+    out("a", 3)
     need("s", e_y)
     g.wait_ge(T.sem.sentg, sent)
     for e in made:

@@ -8,17 +8,17 @@ HF = 2 * CAP
 UW = SL + 8
 ST = 7
 TR = ST * NODES
+SCANNED = (1, 3)
 
 SCRATCH = {
     "snl": ("sbuf", [128, SL // 16], "int32"), "nbl": ("sbuf", [128, 32], "int32"), "dnb": ("dram", [16, 32], "int32"),
-    "nbo": ("sbuf", [128, 32], "uint16"), "nbi": ("sbuf", [128, 32], "uint16"),
+    "nbo": ("sbuf", [128, 32], "uint16"), "nbi": ("sbuf", [128, 16], "uint16"),
     "ill": ("sbuf", [128, 128], "int32"), "ilo": ("sbuf", [128, 128], "uint16"), "dil": ("dram", [16, 128], "int32"),
     "glo": ("sbuf", [128, 32], "uint16"), "gio": ("sbuf", [128, 32], "int32"),
     "pidx": ("sbuf", [128, 1], "int32"), "p12": ("sbuf", [128, 1], "int32"), "ppf": ("sbuf", [128, 1], "float32"),
     "uio": ("sbuf", [128, 8], "int32"), "ui7": ("sbuf", [128, 8], "int32"), "uno": ("sbuf", [128, 8], "uint16"),
-    "yh0": ("sbuf", [128, 128], "float32"), "yh2": ("sbuf", [128, 128], "float32"),
-    "vals": ("sbuf", [128, 512], "int32"), "inv": ("sbuf", [128, SL], "int32"),
-    "iv": ("sbuf", [128, 40], "int32"), "lt": ("sbuf", [128, 40], "uint16"),
+    "vals": ("sbuf", [128, 256], "int32"), "inv": ("sbuf", [128, SL], "int32"),
+    "iv": ("sbuf", [128, 80], "int32"), "ivm": ("sbuf", [128, 40], "int32"), "lt": ("sbuf", [128, 40], "uint16"),
     "xt": ("sbuf", [128, 512], "bfloat16"), "grt": ("sbuf", [128, 512], "bfloat16"),
     "wt": ("sbuf", [128, 2048], "bfloat16"), "w2t": ("sbuf", [128, 2048], "bfloat16"),
     "xg": ("sbuf", [128, 4 * SL], "bfloat16"), "gt": ("sbuf", [128, 4 * SL], "bfloat16"),
@@ -38,7 +38,8 @@ for _b in range(4):
     SCRATCH["z%d" % _b] = ("sbuf", [128, SL], "float32")
     for _n in ("zs", "ma", "mb"):
         SCRATCH["%s%d" % (_n, _b)] = ("sbuf", [128, NODES], "float32")
-    if _b % 2:
+    SCRATCH["yh%d" % _b] = ("sbuf", [128, 128], "float32")
+    if _b in SCANNED:
         SCRATCH["ug%d" % _b] = ("sbuf", [128, F * NODES], "float32")
         SCRATCH["us%d" % _b] = ("sbuf", [128, F * NODES], "float32")
     else:
@@ -87,8 +88,8 @@ def rank_program(g, core, T, topo):
                 e["w"] = True
                 Q[q].wait_ge(e["s"], e["n"])
 
-    def send(src, dst, to, arrived, left):
-        for part in (0, 1):
+    def send(src, dst, to, arrived, left, parts=(0, 1)):
+        for part in parts:
             tr = []
             for i, d in enumerate(to):
                 rid, pid, _ = topo.addr(cores[d])
@@ -110,14 +111,14 @@ def rank_program(g, core, T, topo):
     e_x, e_sn, e_w, e_dnb, e_nb, e_gr, e_inv, e_iln = ev(), ev(), ev(), ev(), ev(), ev(), ev(), ev()
     inc(Y.dma_start(T.xt[:, :], T.x[:, :]), e_x, 16)
     for p in range(4):
-        inc(Y.dma_start(T.snl[16 * p:16 * p + 16, :], T.sn[:, :]), e_sn, 16)
-    for p in range(4, 8):
-        inc(S.dma_start(T.snl[16 * p:16 * p + 16, :], T.sn[:, :]), e_sn, 16)
+        inc((Y, S)[p % 2].dma_start(T.snl[16 * p:16 * p + 16, :], T.sn[:, :]), e_sn, 16)
     for k in range(4):
         inc(S.dma_start(T.dnb[:, 8 * k:8 * k + 8], T.nb[k:16:4, :]), e_dnb, 16)
-    inc(S.dma_start(T.wt[:, :], T.w[:, :]), e_w, 16)
+    for h in range(2):
+        inc(Y.dma_start(T.inv[64 * h:64 * h + 1, :], T.sn[:, :]), e_inv, 16)
+    need("s", e_x)
+    inc(Y.dma_start(T.wt[:, :], T.w[:, :]), e_w, 16)
     inc(Y.dma_start(T.grt[:, :], T.gr[:, :]), e_gr, 16)
-    inc(Y.dma_start(T.inv[0:1, :], T.sn[:, :]), e_inv, 16)
     need("s", e_dnb)
     for p in range(8):
         inc(Y.dma_start(T.nbl[16 * p:16 * p + 16, :], T.dnb[:, :]), e_nb, 16)
@@ -126,26 +127,26 @@ def rank_program(g, core, T, topo):
     e_p, e_zero, e_p12, e_vals = ev(), ev(), ev(), ev()
     inc(g.iota(T.pidx[:, 0:1], [[1, 1]], 0, 129), e_p)
     inc(g.iota(T.gio[:, :], [[1, 4], [16, 8]], 0, 0), e_p)
-    inc(g.iota(T.uio[:, :], [[1, 8]], 0, 8), e_p)
-    inc(g.iota(T.vals[:, 0:2 * NODES], [[2, 2], [ST, NODES]], 4, 0), e_vals)
-    inc(g.iota(T.vals[:, 2 * NODES:4 * NODES], [[-1, 2], [ST, NODES]], 2, 0), e_vals)
+    e_uio = do(g.iota(T.uio[:, :], [[1, 8]], 0, 8))
+    inc(g.iota(T.vals[0:64, :], [[2, 2], [ST, NODES]], NODES + 4, 0), e_uio)
+    need("g", e_p, e_uio)
+    inc(g.iota(T.vals[64:128, :], [[-1, 2], [ST, NODES]], NODES + 2, 0), e_vals)
     inc(V.memset(T.d1[:, 0:4 * TR:ST], 0.0), e_zero)
-    inc(V.memset(T.d0[:, 0:4 * TR:ST], 0.0), e_zero)
     need("v", e_p)
     inc(V.tensor_scalar(T.p12[:, 0:1], T.pidx[:, 0:1], 3 * 128 + 12, None, A.bitwise_and), e_p12)
-    inc(V.tensor_scalar(T.ui7[:, :], T.uio[:, :], 127, None, A.bitwise_and), e_p12)
-    inc(V.memset(T.d0[:, 4:4 * TR:ST], 0.0), e_zero)
+    inc(V.memset(T.d0[:, 0:4 * TR:ST], 0.0), e_zero)
     need("v", e_p12)
     e_ppf = do(V.tensor_copy(T.ppf[:, 0:1], T.p12[:, 0:1]))
-    e_uno = do(V.tensor_copy(T.uno[:, :], T.ui7[:, :]))
-    inc(V.memset(T.d0[:, 6:4 * TR:ST], 0.0), e_zero)
+    inc(V.memset(T.d0[:, 4:4 * TR:ST], 0.0), e_zero)
     need("v", e_ppf)
     e_glo = do(V.tensor_scalar(T.glo[:, :], T.gio[:, :], T.ppf[:, 0:1], None, A.add))
+    inc(V.memset(T.d0[:, 6:4 * TR:ST], 0.0), e_zero)
 
     need("v", e_sn)
     e_so = [ev(), ev(), ev(), ev()]
     for t in (0, 2, 1, 3):
-        inc(V.tensor_scalar(T["so%d" % t][:, :], T.snl[:, :], 4.0, float(t), A.mult, A.add), e_so[t])
+        for h in range(2):
+            inc(V.tensor_scalar(T["so%d" % t][64 * h:64 * h + 64, :], T.snl[0:64, :], 4.0, float(t), A.mult, A.add), e_so[t])
 
     def copy(q, out, src, e):
         return inc(S.activation(out, src, Act.Copy) if q == "a" else V.tensor_copy(out, src), e)
@@ -160,17 +161,22 @@ def rank_program(g, core, T, topo):
 
     need("a", e_x)
     need("v", e_x)
-    for stage, at in enumerate((MATE, FARS)):
-        e_g = ev()
-        for t in (0, 1):
-            need("a", e_so[t])
-            pick("a", t, at, e_g)
-        for t in (2, 3):
-            need("v", e_so[t])
-            pick("v", t, at, e_g)
-        need("v", e_g)
-        need("g", pack("sx", "xg", at))
-        send("sx", "lx", at, T.sem["ax%d" % stage], T.sem.sentx)
+    e_g0, e_g1 = ev(), ev()
+    for q, ts in (("a", (0, 1)), ("v", (2, 3))):
+        for t in ts:
+            need(q, e_so[t])
+            pick(q, t, MATE, e_g0)
+    for t in (0, 1):
+        pick("a", t, FARS, e_g1)
+    pick("v", 2, FARS[:1], e_g1)
+    need("v", e_g0)
+    need("g", pack("sx", "xg", MATE))
+    send("sx", "lx", MATE, T.sem.ax0, T.sem.sentx)
+    pick("v", 2, FARS[1:], e_g1)
+    pick("v", 3, FARS, e_g1)
+    need("v", e_g1)
+    need("g", pack("sx", "xg", FARS))
+    send("sx", "lx", FARS, T.sem.ax1, T.sem.sentx)
 
     e_xo = ev()
     for t in range(4):
@@ -183,30 +189,36 @@ def rank_program(g, core, T, topo):
     e_4 = do(V.tensor_scalar(T.nb4[:, :], T.nbl[:, :], 4, None, A.arith_shift_right))
     e_nbo = do(V.tensor_copy(T.nbo[:, :], T.nbl[:, :]))
     e_56 = do(V.tensor_scalar(T.nb5[:, :], T.nbl[:, :], 40.0, None, A.mult))
+    e_uz = inc(V.memset(T.uu[:, 0:4 * UW:UW], 0.0), e_zero)
     need("v", e_4)
     inc(V.tensor_scalar(T.nb6[:, :], T.nb4[:, :], -639.0, None, A.mult), e_56)
     need("v", e_w)
-    e_wq = do(V.quantize_mx(T.wqc[:, 0:512], T.wqp[:, 0:512], T.wt[:, 0:2048]))
+    e_wq = do(V.quantize_mx(T.wqc[:, 0:256], T.wqp[:, 0:256], T.wt[:, 0:1024]))
     need("v", e_56)
     e = do(V.tensor_tensor(T.nb7[:, :], T.nb5[:, :], T.nb6[:, :], A.add))
     need("v", e_xo)
     e_xoq = pack("lx", "xg", (r,))
     need("v", e)
-    e = do(V.tensor_copy(T.nbi[:, :], T.nb7[:, :]))
-    e_d0 = ev()
-    need("g", e_gp1)
-    for step in (2, 3, 5):
-        inc(g.affine_select(T.d0[:, step:4 * TR:ST], T.d0[:, 1:4 * TR:ST], [[0, 4 * NODES]], A.is_ge, 0.0, 0, 0), e_d0)
+    e = ev()
+    for h in range(2):
+        inc(V.tensor_copy(T.nbi[64 * h:64 * h + 64, :], T.nb7[64 * h:64 * h + 64, 16 * h:16 * h + 16]), e)
+    e_wq2 = do(V.quantize_mx(T.wqc[:, 256:512], T.wqp[:, 256:512], T.wt[:, 1024:2048]))
+    e_d0 = [ev(), ev()]
+    need("g", e_vals, e_gp1)
+    for h in range(2):
+        lo, hi = 2 * TR * h, 2 * TR * (h + 1)
+        for step in (2, 3, 5):
+            inc(g.affine_select(T.d0[:, lo + step:hi:ST], T.d0[:, lo + 1:hi:ST], [[0, 2 * NODES]], A.is_ge, 0.0, 0, 0), e_d0[h])
     e_one = do(g.iota(T.rs[:, :], [[0, F * NODES]], 1, 0, allow_small_or_imprecise_dtypes=True))
     need("g", e_one)
     e_rs = do(g.iota(T.rs[:, 0:F * NODES:F], [[0, NODES]], 0, 0, allow_small_or_imprecise_dtypes=True))
-    e_uz = do(V.memset(T.uu[:, 0:4 * UW:UW], 0.0))
-    need("v", e, e_vals, e_inv)
-    e_sc = do(V.tensor_copy(T.inv[:, 0:SL].indirect(T.nbi[:, 0:32]), T.vals[:, 0:512]))
+    need("v", e, e_uio, e_vals, e_inv)
+    e_sc = do(V.tensor_copy(T.inv[:, 0:SL].indirect(T.nbi[:, 0:16]), T.vals[:, 0:256]))
     e_iv = ev()
     need("s", e_sc)
     for p in range(8):
-        inc(Y.dma_start(T.iv[16 * p:16 * p + 16, :], T.inv[0:1, :]), e_iv, 16)
+        for h in range(2):
+            inc(Y.dma_start(T.iv[16 * p:16 * p + 16, 40 * h:40 * h + 40], T.inv[64 * h:64 * h + 1, :]), e_iv, 16)
 
     g.wait_ge(T.sem.sentx, sent)
 
@@ -223,14 +235,15 @@ def rank_program(g, core, T, topo):
         last[bank] = copy(q, out, T.ps[:, 512 * bank:512 * bank + n], ev())
         return last[bank]
 
-    FIRST = ((0, 0), (1, 0), (0, 1), (1, 1), (2, 0), (2, 1), (3, 0), (3, 1))
     need("t", e_wq, e_xoq)
     TE.wait_ge(T.sem.ax0, arrive(MATE))
     e_m = {}
-    for b, late in FIRST:
-        if (b, late) == (0, 1):
-            TE.wait_ge(T.sem.ax1, arrive(FARS))
-        e_m[b, late] = product("wq", "lx", b, b + 4 * late, FAR if late else NEAR, HF)
+    for b in (0, 1):
+        e_m[b, 0] = product("wq", "lx", b, b, NEAR, HF)
+    TE.wait_ge(T.sem.ax1, arrive(FARS))
+    e_m[0, 1] = product("wq", "lx", 0, 4, FAR, CAP)
+    e_m[0, 2] = product("wq", "lx", 0, 7, FAR + CAP, CAP)
+    e_m[1, 1] = product("wq", "lx", 1, 5, FAR, HF)
     need("s", e_m[0, 1])
     inc(Y.dma_start(T.w2t[:, :], T.w2[:, :]), e_w2, 16)
     for f in range(F):
@@ -246,9 +259,9 @@ def rank_program(g, core, T, topo):
     def nbr(b, k):
         return T["z%d" % b][:, 0:SL].indirect(T.nbo[:, 8 * k:8 * k + 8])
 
-    def zcopy(b, late):
+    def zcopy(q, b, late):
         a = FAR if late else NEAR
-        e_z[b].append(take("a", b + 4 * late, T["z%d" % b][:, a:a + HF], HF, e_m[b, late]))
+        e_z[b].append(take(q, b + 4 * late, T["z%d" % b][:, a:a + HF], HF, e_m[b, late]))
 
     def zs(b):
         need("a", e_nbo, *e_z[b])
@@ -276,53 +289,62 @@ def rank_program(g, core, T, topo):
         need("v", e_mb[b])
         e_w3[b] = do(V.tensor_tensor(mask(b, 1), nbr(b, 3), T["mb%d" % b][:, :], A.is_gt))
 
+    def affine(b, to, src, scale, bias):
+        if b < 3:
+            inc(S.activation(mask(b, to), mask(b, src), Act.Identity, bias=bias, scale=scale), e_k[b])
+        else:
+            inc(V.tensor_scalar(mask(b, to), mask(b, src), scale, bias, A.mult, A.add), e_k[b])
+
     def n2(b):
-        need("v", e_p2[b])
-        inc(V.tensor_scalar(mask(b, 6), mask(b, 2), -1.0, 1.0, A.mult, A.add), e_k[b])
+        need("a" if b < 3 else "v", e_p2[b])
+        affine(b, 6, 2, -1.0, 1.0)
 
     def n3(b):
-        need("v", e_w3[b])
+        need("a" if b < 3 else "v", e_w3[b])
         for step in (3, 5):
-            inc(V.tensor_scalar(mask(b, step), mask(b, 1), -1.0, None, A.add), e_k[b])
+            affine(b, step, 1, 1.0, -1.0)
 
     def ch(b):
-        need("v", e_zero, e_d0, e_k[b])
+        need("v", e_zero, e_d0[b // 2], e_k[b])
         e_ch[b] = do(V.tensor_tensor_scan(T.gb[:, TR * b:TR * b + TR], T.d0[:, TR * b:TR * b + TR], T.d1[:, TR * b:TR * b + TR], 0.0, A.subtract, A.mult))
 
     def grad(q, b, lo, hi, e):
         need(q, e_lt, e_ch[b])
         copy(q, T.gt[:, 4 * lo + b:4 * hi:4], T.gb[:, TR * b:TR * b + TR].indirect(T.lt[:, lo // 16:hi // 16]), e)
 
-    for b, late in FIRST:
-        zcopy(b, late)
-        if late:
-            zs(b)
+    def near(b):
+        zcopy("a", b, 0)
+
+    def late(b):
+        if b == 0:
+            e_z[0].append(take("a", 4, T.z0[:, FAR:FAR + CAP], CAP, e_m[0, 1]))
+            e_z[0].append(take("v", 7, T.z0[:, FAR + CAP:FAR + HF], CAP, e_m[0, 2]))
+            need("t", e_wq2)
+            for c, h in ((2, 0), (2, 1), (3, 0), (3, 1)):
+                e_m[c, h] = product("wq", "lx", c, c + 4 * h, FAR if h else NEAR, HF)
+        else:
+            zcopy("v" if b == 1 else "a", b, 1)
+
+    def whole(b):
+        grad("a", b, 0, SL, e_gf0)
+
     e_gf, e_gp, e_go, e_gf0, e_p2, e_w3 = ev(), ev(), ev(), ev(), {}, {}
-    for b in range(4):
-        if b == 0:
-            m01(b)
-            q0(b)
-            m012(b)
-        p2(b)
-        w3(b)
-        if b == 3:
-            q0(b)
-        n2(b)
-        if b < 3:
-            m01(b + 1)
-        n3(b)
-        if b < 2:
-            q0(b + 1)
-        if b < 3:
-            m012(b + 1)
-        ch(b)
-        if b == 0:
-            need("v", e_iv)
-            e_lt = do(V.tensor_copy(T.lt[:, :], T.iv[:, :]))
-        if b < 2:
-            grad("a", b, 0, SL, e_gf0)
-    grad("a", 2, PART, PART + CAP, e_gp)
+    for step, b in ((near, 0), (near, 1), (late, 0), (late, 1), (zs, 0), (zs, 1), (near, 2), (late, 2),
+                    (m01, 0), (q0, 0), (m012, 0), (p2, 0), (m01, 1), (w3, 0), (q0, 1), (zs, 2), (n2, 0), (m012, 1), (n3, 0),
+                    (near, 3), (late, 3), (p2, 1), (m01, 2), (ch, 0)):
+        step(b)
+    w3(1)
+    need("v", e_iv)
+    e = do(V.tensor_tensor(T.ivm[:, :], T.iv[:, 0:40], T.iv[:, 40:80], A.max))
+    q0(2)
+    need("v", e)
+    e_lt = do(V.tensor_scalar(T.lt[:, :], T.ivm[:, :], -float(NODES), None, A.add))
+    for step, b in ((zs, 3), (n2, 1), (m012, 2), (n3, 1), (whole, 0), (p2, 2), (m01, 3), (ch, 1),
+                    (w3, 2), (p2, 3), (n2, 2), (m012, 3), (n3, 2), (whole, 1), (q0, 3), (w3, 3), (ch, 2), (n2, 3), (n3, 3)):
+        step(b)
     grad("a", 2, FAR, FAR + HF, e_gf)
+    grad("v", 2, PART, PART + CAP, e_gp)
+    ch(3)
     grad("v", 3, PART, PART + CAP, e_gp)
     grad("a", 3, FAR, FAR + HF, e_gf)
     need("v", e_gf0, e_gp)
@@ -338,8 +360,12 @@ def rank_program(g, core, T, topo):
     e_vq = do(V.quantize_mx(T.vqc[:, 0:512], T.vqp[:, 0:512], T.w2t[:, 0:2048]))
     need("v", e_go)
     e_goq = pack("lg", "gt", (r,))
+    need("v", e_uio)
+    e = do(V.tensor_scalar(T.ui7[:, :], T.uio[:, :], 127, None, A.bitwise_and))
     need("v", e_iln)
     e_ilo = do(V.tensor_scalar(T.ilo[:, :], T.ill[:, :], 1.0, None, A.add))
+    need("v", e)
+    e_uno = do(V.tensor_copy(T.uno[:, :], T.ui7[:, :]))
 
     e_u = {b: [e_uz] for b in range(4)}
     e_ac, e_ug, e_us, e_yh, e_y = {}, {}, {}, {}, ev()
@@ -378,7 +404,7 @@ def rank_program(g, core, T, topo):
 
     def out(q, b):
         e = ev()
-        if b % 2:
+        if b in SCANNED:
             need(q, e_us[b])
             copy(q, T["yo%d" % b][:, :], T["us%d" % b][:, F - 1:F * NODES:F], e)
         else:

@@ -11,8 +11,8 @@ TR = ST * NODES
 SCANNED = (1, 3)
 
 SCRATCH = {
-    "snl": ("sbuf", [128, SL // 16], "int32"), "nbl": ("sbuf", [128, 32], "int32"), "dnb": ("dram", [16, 32], "int32"),
-    "nbo": ("sbuf", [128, 32], "uint16"), "nbi": ("sbuf", [128, 16], "uint16"),
+    "snl": ("sbuf", [128, SL // 16], "int32"), "nbl": ("sbuf", [128, 64], "int32"), "dnb": ("dram", [16, 64], "int32"),
+    "two": ("sbuf", [128, 64], "int32"), "nbo": ("sbuf", [128, 64], "uint16"), "nbi": ("sbuf", [128, 16], "uint16"),
     "ill": ("sbuf", [128, 128], "int32"), "ilo": ("sbuf", [128, 128], "uint16"), "dil": ("dram", [16, 128], "int32"),
     "glo": ("sbuf", [128, 32], "uint16"), "gio": ("sbuf", [128, 32], "int32"),
     "pidx": ("sbuf", [128, 1], "int32"), "p12": ("sbuf", [128, 1], "int32"), "ppf": ("sbuf", [128, 1], "float32"),
@@ -25,19 +25,18 @@ SCRATCH = {
     "d0": ("sbuf", [128, 4 * TR], "bfloat16"), "d1": ("sbuf", [128, 4 * TR], "bfloat16"),
     "gb": ("sbuf", [128, 4 * TR], "bfloat16"),
     "rs": ("sbuf", [128, F * NODES], "bfloat16"),
+    "zz": ("sbuf", [128, 4 * SL], "float32"), "zs": ("sbuf", [128, 4 * NODES], "float32"),
+    "ma": ("sbuf", [128, 4 * NODES], "float32"), "mb": ("sbuf", [128, 4 * NODES], "float32"),
     "uu": ("sbuf", [128, 4 * UW], "float32"),
     "ps": ("psum", [128, 4096], "float32"),
 }
-for _i in range(4, 8):
-    SCRATCH["nb%d" % _i] = ("sbuf", [128, 32], "int32")
+for _i in range(4, 9):
+    SCRATCH["nb%d" % _i] = ("sbuf", [128, 64], "int32")
 for _n, _w in (("wq", 512), ("vq", 512), ("sx", SL), ("sg", SL), ("lx", SL), ("lg", SL)):
     SCRATCH[_n + "c"] = ("sbuf", [128, _w], "float8_e4m3fn_x4")
     SCRATCH[_n + "p"] = ("sbuf", [128, _w], "uint8")
 for _b in range(4):
     SCRATCH["so%d" % _b] = ("sbuf", [128, SL // 16], "uint16")
-    SCRATCH["z%d" % _b] = ("sbuf", [128, SL], "float32")
-    for _n in ("zs", "ma", "mb"):
-        SCRATCH["%s%d" % (_n, _b)] = ("sbuf", [128, NODES], "float32")
     SCRATCH["yh%d" % _b] = ("sbuf", [128, 128], "float32")
     if _b in SCANNED:
         SCRATCH["ug%d" % _b] = ("sbuf", [128, F * NODES], "float32")
@@ -47,8 +46,8 @@ for _b in range(4):
             SCRATCH["ac%d%d" % (_b, _k)] = ("sbuf", [128, 256], "float32")
     SCRATCH["yo%d" % _b] = ("sbuf", [128, 128], "float32")
 
-EVENTS = 144
-SEMAPHORES = ["ax0", "ax1", "ag0", "ag1", "sentx", "sentg"] + ["e%d" % _i for _i in range(EVENTS)]
+EVENTS = 145
+SEMAPHORES = ["ax0", "ax1", "ag0", "ag1", "sent"] + ["e%d" % _i for _i in range(EVENTS)]
 
 
 def rank_program(g, core, T, topo):
@@ -88,8 +87,8 @@ def rank_program(g, core, T, topo):
                 e["w"] = True
                 Q[q].wait_ge(e["s"], e["n"])
 
-    def send(src, dst, to, arrived, left, parts=(0, 1)):
-        for part in parts:
+    def send(src, dst, to, arrived):
+        for part in (0, 1):
             tr = []
             for i, d in enumerate(to):
                 rid, pid, _ = topo.addr(cores[d])
@@ -101,7 +100,7 @@ def rank_program(g, core, T, topo):
                     f, t = T[src + "p"][:, a:a + CAP], T[dst + "p"][:, b:b + CAP]
                 tr.append(RemoteDMATransfer(dst_ids=[DstId(rid=rid, pnc=pid)], dma_engine_mask=sum(1 << e for e in es),
                                             remote_sem=arrived, src=f, dst=t))
-            g.remote_dma_fused(tr, local_sem=left)
+            g.remote_dma_fused(tr, local_sem=T.sem.sent)
 
     def arrive(at):
         return sum(len(topo.engines(cores[s], cores[r])) for s in at)
@@ -109,27 +108,28 @@ def rank_program(g, core, T, topo):
     sent = sum(len(topo.engines(cores[r], cores[d])) for d in MATE + FARS)
 
     e_x, e_sn, e_w, e_dnb, e_nb, e_gr, e_inv, e_iln = ev(), ev(), ev(), ev(), ev(), ev(), ev(), ev()
-    inc(Y.dma_start(T.xt[:, :], T.x[:, :]), e_x, 16)
     for p in range(4):
         inc((Y, S)[p % 2].dma_start(T.snl[16 * p:16 * p + 16, :], T.sn[:, :]), e_sn, 16)
+    inc(Y.dma_start(T.xt[:, :], T.x[:, :]), e_x, 16)
     for k in range(4):
-        inc(S.dma_start(T.dnb[:, 8 * k:8 * k + 8], T.nb[k:16:4, :]), e_dnb, 16)
-    for h in range(2):
-        inc(Y.dma_start(T.inv[64 * h:64 * h + 1, :], T.sn[:, :]), e_inv, 16)
-    need("s", e_x)
+        for h in range(2):
+            inc((S, Y)[h].dma_start(T.dnb[:, 16 * k + 8 * h:16 * k + 8 * h + 8], T.nb[k:16:4, :]), e_dnb, 16)
     inc(Y.dma_start(T.wt[:, :], T.w[:, :]), e_w, 16)
     inc(Y.dma_start(T.grt[:, :], T.gr[:, :]), e_gr, 16)
+    for h in range(2):
+        inc(Y.dma_start(T.inv[64 * h:64 * h + 1, :], T.sn[:, :]), e_inv, 16)
     need("s", e_dnb)
-    for p in range(8):
+    for p in range(4):
         inc(Y.dma_start(T.nbl[16 * p:16 * p + 16, :], T.dnb[:, :]), e_nb, 16)
     e_dil, e_w2 = ev(), ev()
 
     e_p, e_zero, e_p12, e_vals = ev(), ev(), ev(), ev()
     inc(g.iota(T.pidx[:, 0:1], [[1, 1]], 0, 129), e_p)
-    inc(g.iota(T.gio[:, :], [[1, 4], [16, 8]], 0, 0), e_p)
+    e_gio = do(g.iota(T.gio[:, :], [[1, 4], [16, 8]], 0, 0))
     e_uio = do(g.iota(T.uio[:, :], [[1, 8]], 0, 8))
+    inc(g.iota(T.two[:, :], [[0, 4], [SL, 2], [0, 8]], 0, 0), e_uio)
     inc(g.iota(T.vals[0:64, :], [[2, 2], [ST, NODES]], NODES + 4, 0), e_uio)
-    need("g", e_p, e_uio)
+    need("g", e_p, e_gio, e_uio)
     inc(g.iota(T.vals[64:128, :], [[-1, 2], [ST, NODES]], NODES + 2, 0), e_vals)
     inc(V.memset(T.d1[:, 0:4 * TR:ST], 0.0), e_zero)
     need("v", e_p)
@@ -138,9 +138,6 @@ def rank_program(g, core, T, topo):
     need("v", e_p12)
     e_ppf = do(V.tensor_copy(T.ppf[:, 0:1], T.p12[:, 0:1]))
     inc(V.memset(T.d0[:, 4:4 * TR:ST], 0.0), e_zero)
-    need("v", e_ppf)
-    e_glo = do(V.tensor_scalar(T.glo[:, :], T.gio[:, :], T.ppf[:, 0:1], None, A.add))
-    inc(V.memset(T.d0[:, 6:4 * TR:ST], 0.0), e_zero)
 
     need("v", e_sn)
     e_so = [ev(), ev(), ev(), ev()]
@@ -151,8 +148,8 @@ def rank_program(g, core, T, topo):
     def copy(q, out, src, e):
         return inc(S.activation(out, src, Act.Copy) if q == "a" else V.tensor_copy(out, src), e)
 
-    def pick(q, t, at, e):
-        lo, hi = CAP * at[0], CAP * (at[-1] + 1)
+    def pick(q, t, at, e, a=0, b=None):
+        lo, hi = CAP * at[0] + a, CAP * at[0] + (b or CAP * len(at))
         copy(q, T.xg[:, 4 * lo + t:4 * hi:4], T.xt[:, 0:512].indirect(T["so%d" % t][:, lo // 16:hi // 16]), e)
 
     def pack(dst, src, at):
@@ -168,15 +165,18 @@ def rank_program(g, core, T, topo):
             pick(q, t, MATE, e_g0)
     for t in (0, 1):
         pick("a", t, FARS, e_g1)
-    pick("v", 2, FARS[:1], e_g1)
+    pick("v", 2, FARS, e_g1, 0, CAP)
     need("v", e_g0)
     need("g", pack("sx", "xg", MATE))
-    send("sx", "lx", MATE, T.sem.ax0, T.sem.sentx)
-    pick("v", 2, FARS[1:], e_g1)
+    send("sx", "lx", MATE, T.sem.ax0)
+    pick("v", 2, FARS, e_g1, CAP, HF)
     pick("v", 3, FARS, e_g1)
+    need("v", e_ppf, e_gio)
+    e_glo = do(V.tensor_scalar(T.glo[:, :], T.gio[:, :], T.ppf[:, 0:1], None, A.add))
+    inc(V.memset(T.d0[:, 6:3 * TR:ST], 0.0), e_zero)
     need("v", e_g1)
     need("g", pack("sx", "xg", FARS))
-    send("sx", "lx", FARS, T.sem.ax1, T.sem.sentx)
+    send("sx", "lx", FARS, T.sem.ax1)
 
     e_xo = ev()
     for t in range(4):
@@ -185,23 +185,27 @@ def rank_program(g, core, T, topo):
     e_ch = {}
     need("a", e_gr, e_glo)
     e_gp1 = copy("a", T.d0[:, 1:4 * TR:ST], T.grt[:, 0:512].indirect(T.glo[:, 0:32]), ev())
-    need("v", e_nb)
-    e_4 = do(V.tensor_scalar(T.nb4[:, :], T.nbl[:, :], 4, None, A.arith_shift_right))
-    e_nbo = do(V.tensor_copy(T.nbo[:, :], T.nbl[:, :]))
-    e_56 = do(V.tensor_scalar(T.nb5[:, :], T.nbl[:, :], 40.0, None, A.mult))
+    need("v", e_nb, e_uio)
+    e_4 = do(V.tensor_scalar(T.nb4[0:64, :], T.nbl[0:64, :], 4, None, A.arith_shift_right))
+    inc(V.tensor_tensor(T.nb8[0:64, :], T.nbl[0:64, :], T.two[0:64, :], A.add), e_4)
+    e_56 = do(V.tensor_scalar(T.nb5[0:64, :], T.nbl[0:64, :], 40.0, None, A.mult))
+    inc(V.memset(T.d0[:, 3 * TR + 6:4 * TR:ST], 0.0), e_zero)
     e_uz = inc(V.memset(T.uu[:, 0:4 * UW:UW], 0.0), e_zero)
     need("v", e_4)
-    inc(V.tensor_scalar(T.nb6[:, :], T.nb4[:, :], -639.0, None, A.mult), e_56)
+    inc(V.tensor_scalar(T.nb6[0:64, :], T.nb4[0:64, :], -639.0, None, A.mult), e_56)
+    e_nbo = ev()
+    for h in range(2):
+        inc(V.tensor_copy(T.nbo[64 * h:64 * h + 64, :], T.nb8[0:64, :]), e_nbo)
     need("v", e_w)
     e_wq = do(V.quantize_mx(T.wqc[:, 0:256], T.wqp[:, 0:256], T.wt[:, 0:1024]))
     need("v", e_56)
-    e = do(V.tensor_tensor(T.nb7[:, :], T.nb5[:, :], T.nb6[:, :], A.add))
+    e = do(V.tensor_tensor(T.nb7[0:64, :], T.nb5[0:64, :], T.nb6[0:64, :], A.add))
     need("v", e_xo)
     e_xoq = pack("lx", "xg", (r,))
     need("v", e)
     e = ev()
     for h in range(2):
-        inc(V.tensor_copy(T.nbi[64 * h:64 * h + 64, :], T.nb7[64 * h:64 * h + 64, 16 * h:16 * h + 16]), e)
+        inc(V.tensor_copy(T.nbi[64 * h:64 * h + 64, :], T.nb7[0:64, 32 * h + 8:32 * h + 24]), e)
     e_wq2 = do(V.quantize_mx(T.wqc[:, 256:512], T.wqp[:, 256:512], T.wt[:, 1024:2048]))
     e_d0 = [ev(), ev()]
     need("g", e_vals, e_gp1)
@@ -209,18 +213,16 @@ def rank_program(g, core, T, topo):
         lo, hi = 2 * TR * h, 2 * TR * (h + 1)
         for step in (2, 3, 5):
             inc(g.affine_select(T.d0[:, lo + step:hi:ST], T.d0[:, lo + 1:hi:ST], [[0, 2 * NODES]], A.is_ge, 0.0, 0, 0), e_d0[h])
-    e_one = do(g.iota(T.rs[:, :], [[0, F * NODES]], 1, 0, allow_small_or_imprecise_dtypes=True))
-    need("g", e_one)
-    e_rs = do(g.iota(T.rs[:, 0:F * NODES:F], [[0, NODES]], 0, 0, allow_small_or_imprecise_dtypes=True))
+    e_rs = do(g.iota(T.rs[:, :], [[0, F * NODES]], 1, 0, allow_small_or_imprecise_dtypes=True))
+    need("g", e_rs)
+    inc(g.iota(T.rs[:, 0:F * NODES:F], [[0, NODES]], 0, 0, allow_small_or_imprecise_dtypes=True), e_rs)
     need("v", e, e_uio, e_vals, e_inv)
     e_sc = do(V.tensor_copy(T.inv[:, 0:SL].indirect(T.nbi[:, 0:16]), T.vals[:, 0:256]))
     e_iv = ev()
     need("s", e_sc)
-    for p in range(8):
+    for p in range(4):
         for h in range(2):
             inc(Y.dma_start(T.iv[16 * p:16 * p + 16, 40 * h:40 * h + 40], T.inv[64 * h:64 * h + 1, :]), e_iv, 16)
-
-    g.wait_ge(T.sem.sentx, sent)
 
     last = {}
 
@@ -244,132 +246,167 @@ def rank_program(g, core, T, topo):
     e_m[0, 1] = product("wq", "lx", 0, 4, FAR, CAP)
     e_m[0, 2] = product("wq", "lx", 0, 7, FAR + CAP, CAP)
     e_m[1, 1] = product("wq", "lx", 1, 5, FAR, HF)
+    need("t", e_wq2)
+    for b, late in ((2, 1), (2, 0), (3, 0)):
+        e_m[b, late] = product("wq", "lx", b, b + 4 * late, FAR if late else NEAR, HF)
     need("s", e_m[0, 1])
     inc(Y.dma_start(T.w2t[:, :], T.w2[:, :]), e_w2, 16)
     for f in range(F):
         inc(Y.dma_start(T.dil[:, 8 * f:8 * f + 8], T.il[f:16:F, :]), e_dil, 16)
     inc(Y.dma_start(T.dil[:, 64:128], T.il[:, :]), e_dil, 16)
     need("s", e_dil)
-    for p in range(8):
+    for p in range(4):
         inc(Y.dma_start(T.ill[16 * p:16 * p + 16, :], T.dil[:, :]), e_iln, 16)
 
     e_z = {b: [] for b in range(4)}
-    e_zs, e_ma, e_mb, e_k = {}, {}, {}, {b: ev() for b in range(4)}
+    e_zs, e_ma, e_mb, e_p2, e_w3, e_k = ({b: [] for b in range(4)} for _ in range(6))
 
-    def nbr(b, k):
-        return T["z%d" % b][:, 0:SL].indirect(T.nbo[:, 8 * k:8 * k + 8])
+    def nbr(bs, k):
+        return T.zz[:, SL * bs[0]:SL * (bs[-1] + 1)].indirect(T.nbo[:, 16 * k:16 * k + 8 * len(bs)])
+
+    def node(name, bs):
+        return T[name][:, NODES * bs[0]:NODES * (bs[-1] + 1)]
+
+    def mask(bs, step):
+        return T.d1[:, TR * bs[0] + step:TR * (bs[-1] + 1):ST]
+
+    def after(q, d, bs):
+        for b in bs:
+            need(q, *d[b])
+
+    def gave(d, bs, *ops):
+        e = ev()
+        for op in ops:
+            inc(op, e)
+        for b in bs:
+            d[b].append(e)
 
     def zcopy(q, b, late):
-        a = FAR if late else NEAR
-        e_z[b].append(take(q, b + 4 * late, T["z%d" % b][:, a:a + HF], HF, e_m[b, late]))
+        a = SL * b + (FAR if late else NEAR)
+        e_z[b].append(take(q, b + 4 * late, T.zz[:, a:a + HF], HF, e_m[b, late]))
 
-    def zs(b):
-        need("a", e_nbo, *e_z[b])
-        e_zs[b] = do(S.activation(T["zs%d" % b][:, :], nbr(b, 1), Act.Copy))
+    def zs(*bs):
+        need("a", e_nbo)
+        after("a", e_z, bs)
+        gave(e_zs, bs, S.activation(node("zs", bs), nbr(bs, 1), Act.Copy))
 
-    def mask(b, step):
-        return T.d1[:, TR * b + step:TR * b + TR:ST]
+    def m01(*bs):
+        need("v", e_nbo)
+        after("v", e_zs, bs)
+        after("v", e_z, bs)
+        gave(e_ma, bs, V.tensor_tensor(node("ma", bs), nbr(bs, 0), node("zs", bs), A.max))
 
-    def m01(b):
-        need("v", e_nbo, e_zs[b], *e_z[b])
-        e_ma[b] = do(V.tensor_tensor(T["ma%d" % b][:, :], nbr(b, 0), T["zs%d" % b][:, :], A.max))
+    def q0(*bs):
+        gave(e_k, bs, V.tensor_tensor(mask(bs, 4), nbr(bs, 0), node("zs", bs), A.is_ge))
 
-    def q0(b):
-        inc(V.tensor_tensor(mask(b, 4), nbr(b, 0), T["zs%d" % b][:, :], A.is_ge), e_k[b])
+    def m012(*bs):
+        after("v", e_ma, bs)
+        gave(e_mb, bs, V.tensor_tensor(node("mb", bs), nbr(bs, 2), node("ma", bs), A.max))
 
-    def m012(b):
-        need("v", e_ma[b])
-        e_mb[b] = do(V.tensor_tensor(T["mb%d" % b][:, :], nbr(b, 2), T["ma%d" % b][:, :], A.max))
+    def p2(*bs):
+        after("v", e_ma, bs)
+        gave(e_p2, bs, V.tensor_tensor(mask(bs, 2), nbr(bs, 2), node("ma", bs), A.is_gt))
 
-    def p2(b):
-        need("v", e_ma[b])
-        e_p2[b] = do(V.tensor_tensor(mask(b, 2), nbr(b, 2), T["ma%d" % b][:, :], A.is_gt))
+    def w3(*bs):
+        after("v", e_mb, bs)
+        gave(e_w3, bs, V.tensor_tensor(mask(bs, 1), nbr(bs, 3), node("mb", bs), A.is_gt))
 
-    def w3(b):
-        need("v", e_mb[b])
-        e_w3[b] = do(V.tensor_tensor(mask(b, 1), nbr(b, 3), T["mb%d" % b][:, :], A.is_gt))
+    def affine(q, bs, to, src, scale, bias):
+        if q == "a":
+            return S.activation(mask(bs, to), mask(bs, src), Act.Identity, bias=bias, scale=scale)
+        return V.tensor_scalar(mask(bs, to), mask(bs, src), scale, bias, A.mult, A.add)
 
-    def affine(b, to, src, scale, bias):
-        if b < 3:
-            inc(S.activation(mask(b, to), mask(b, src), Act.Identity, bias=bias, scale=scale), e_k[b])
-        else:
-            inc(V.tensor_scalar(mask(b, to), mask(b, src), scale, bias, A.mult, A.add), e_k[b])
+    def n2(q, *bs):
+        after(q, e_p2, bs)
+        gave(e_k, bs, affine(q, bs, 6, 2, -1.0, 1.0))
 
-    def n2(b):
-        need("a" if b < 3 else "v", e_p2[b])
-        affine(b, 6, 2, -1.0, 1.0)
-
-    def n3(b):
-        need("a" if b < 3 else "v", e_w3[b])
-        for step in (3, 5):
-            affine(b, step, 1, 1.0, -1.0)
+    def n3(q, *bs):
+        after(q, e_w3, bs)
+        gave(e_k, bs, affine(q, bs, 3, 1, 1.0, -1.0), affine(q, bs, 5, 1, 1.0, -1.0))
 
     def ch(b):
-        need("v", e_zero, e_d0[b // 2], e_k[b])
+        need("v", e_zero, e_d0[b // 2], *e_k[b])
         e_ch[b] = do(V.tensor_tensor_scan(T.gb[:, TR * b:TR * b + TR], T.d0[:, TR * b:TR * b + TR], T.d1[:, TR * b:TR * b + TR], 0.0, A.subtract, A.mult))
 
     def grad(q, b, lo, hi, e):
         need(q, e_lt, e_ch[b])
         copy(q, T.gt[:, 4 * lo + b:4 * hi:4], T.gb[:, TR * b:TR * b + TR].indirect(T.lt[:, lo // 16:hi // 16]), e)
 
-    def near(b):
-        zcopy("a", b, 0)
-
-    def late(b):
-        if b == 0:
-            e_z[0].append(take("a", 4, T.z0[:, FAR:FAR + CAP], CAP, e_m[0, 1]))
-            e_z[0].append(take("v", 7, T.z0[:, FAR + CAP:FAR + HF], CAP, e_m[0, 2]))
-            need("t", e_wq2)
-            for c, h in ((2, 0), (2, 1), (3, 0), (3, 1)):
-                e_m[c, h] = product("wq", "lx", c, c + 4 * h, FAR if h else NEAR, HF)
-        else:
-            zcopy("v" if b == 1 else "a", b, 1)
-
-    def whole(b):
-        grad("a", b, 0, SL, e_gf0)
-
-    e_gf, e_gp, e_go, e_gf0, e_p2, e_w3 = ev(), ev(), ev(), ev(), {}, {}
-    for step, b in ((near, 0), (near, 1), (late, 0), (late, 1), (zs, 0), (zs, 1), (near, 2), (late, 2),
-                    (m01, 0), (q0, 0), (m012, 0), (p2, 0), (m01, 1), (w3, 0), (q0, 1), (zs, 2), (n2, 0), (m012, 1), (n3, 0),
-                    (near, 3), (late, 3), (p2, 1), (m01, 2), (ch, 0)):
-        step(b)
-    w3(1)
+    e_gf, e_gp, e_go, e_gf0 = ev(), ev(), ev(), ev()
+    zcopy("a", 0, 0)
+    zcopy("a", 1, 0)
+    e_z[0].append(take("a", 4, T.zz[:, FAR:FAR + CAP], CAP, e_m[0, 1]))
+    e_z[0].append(take("v", 7, T.zz[:, FAR + CAP:FAR + HF], CAP, e_m[0, 2]))
+    e_m[3, 1] = product("wq", "lx", 3, 7, FAR, HF)
+    zcopy("v", 1, 1)
+    zcopy("v", 2, 1)
+    zs(0)
+    zs(1)
+    for b, late in ((2, 0), (3, 0), (3, 1)):
+        zcopy("a", b, late)
+    zs(2, 3)
+    for b in (0, 1):
+        m01(b)
+        q0(b)
+    m012(0, 1)
+    p2(0, 1)
+    w3(0, 1)
+    n2("a", 0, 1)
+    m01(2, 3)
+    n3("a", 0)
+    n3("a", 1)
     need("v", e_iv)
-    e = do(V.tensor_tensor(T.ivm[:, :], T.iv[:, 0:40], T.iv[:, 40:80], A.max))
-    q0(2)
+    e = do(V.tensor_tensor(T.ivm[0:64, :], T.iv[0:64, 0:40], T.iv[0:64, 40:80], A.max))
+    q0(2, 3)
     need("v", e)
-    e_lt = do(V.tensor_scalar(T.lt[:, :], T.ivm[:, :], -float(NODES), None, A.add))
-    for step, b in ((zs, 3), (n2, 1), (m012, 2), (n3, 1), (whole, 0), (p2, 2), (m01, 3), (ch, 1),
-                    (w3, 2), (p2, 3), (n2, 2), (m012, 3), (n3, 2), (whole, 1), (q0, 3), (w3, 3), (ch, 2), (n2, 3), (n3, 3)):
-        step(b)
+    e_lt = ev()
+    for h in range(2):
+        inc(V.tensor_scalar(T.lt[64 * h:64 * h + 64, :], T.ivm[0:64, :], -float(NODES), None, A.add), e_lt)
+    ch(0)
+    grad("a", 0, 0, SL, e_gf0)
+    m012(2, 3)
+    p2(2, 3)
+    ch(1)
+    n2("a", 2, 3)
+    w3(2)
+    grad("a", 1, 0, SL, e_gf0)
+    w3(3)
+    n3("v", 2)
+    n3("v", 3)
+    ch(2)
     grad("a", 2, FAR, FAR + HF, e_gf)
-    grad("v", 2, PART, PART + CAP, e_gp)
     ch(3)
+    grad("v", 2, PART, PART + CAP, e_gp)
     grad("v", 3, PART, PART + CAP, e_gp)
-    grad("a", 3, FAR, FAR + HF, e_gf)
+    grad("a", 3, FAR, FAR + HF - 64, e_gf)
+    grad("v", 3, FAR + HF - 64, FAR + HF, e_gf)
+    need("v", e_w2)
+    e_vq = do(V.quantize_mx(T.vqc[:, 0:128], T.vqp[:, 0:128], T.w2t[:, 0:512]))
     need("v", e_gf0, e_gp)
     need("g", pack("sg", "gt", MATE))
-    send("sg", "lg", MATE, T.sem.ag1, T.sem.sentg)
+    send("sg", "lg", MATE, T.sem.ag1)
     need("v", e_gf)
     need("g", pack("sg", "gt", FARS))
-    send("sg", "lg", FARS, T.sem.ag0, T.sem.sentg)
+    send("sg", "lg", FARS, T.sem.ag0)
 
     for b in (2, 3):
         grad("a", b, OWN, OWN + CAP, e_go)
-    need("v", e_w2)
-    e_vq = do(V.quantize_mx(T.vqc[:, 0:512], T.vqp[:, 0:512], T.w2t[:, 0:2048]))
+    inc(V.quantize_mx(T.vqc[:, 128:512], T.vqp[:, 128:512], T.w2t[:, 512:2048]), e_vq)
     need("v", e_go)
     e_goq = pack("lg", "gt", (r,))
     need("v", e_uio)
     e = do(V.tensor_scalar(T.ui7[:, :], T.uio[:, :], 127, None, A.bitwise_and))
     need("v", e_iln)
-    e_ilo = do(V.tensor_scalar(T.ilo[:, :], T.ill[:, :], 1.0, None, A.add))
+    e_ilo = ev()
+    for h in range(2):
+        inc(V.tensor_scalar(T.ilo[64 * h:64 * h + 64, :], T.ill[0:64, :], 1.0, None, A.add), e_ilo)
     need("v", e)
     e_uno = do(V.tensor_copy(T.uno[:, :], T.ui7[:, :]))
 
     e_u = {b: [e_uz] for b in range(4)}
     e_ac, e_ug, e_us, e_yh, e_y = {}, {}, {}, {}, ev()
-    RUN = {"o": (OWN, CAP, 0), "f": (FAR, HF, 4), "p": (PART, CAP, 0)}
+    RUN = {"o": (OWN, CAP, 0), "f": (FAR, HF, 0), "p": (PART, CAP, 4), "f0": (FAR, CAP, 0), "f1": (FAR + CAP, CAP, 4),
+           "g0": (FAR, HF - 128, 0), "g1": (FAR + HF - 128, 128, 2)}
 
     def mult(b, run):
         a, n, bank = RUN[run]
@@ -410,8 +447,9 @@ def rank_program(g, core, T, topo):
         else:
             need(q, e_ac[b], e_yh[b])
             inc(V.tensor_tensor(T["yo%d" % b][:, :], T["ac%d3" % b][:, 0:128].indirect(T.uno[:, :]), T["yh%d" % b][:, :], A.add), e)
-        need("s", e)
-        inc(Y.dma_start(T.y[:, 128 * b:128 * b + 128], T["yo%d" % b][:, :]), e_y, 16)
+        dq = "a" if b == 3 else "s"
+        need(dq, e)
+        inc(Q[dq].dma_start(T.y[:, 128 * b:128 * b + 128], T["yo%d" % b][:, :]), e_y, 16)
 
     need("t", e_vq, e_goq)
     for b in (0, 2, 1, 3):
@@ -424,17 +462,21 @@ def rank_program(g, core, T, topo):
     for b in (0, 2, 1, 3):
         mult(b, "p")
     TE.wait_ge(T.sem.ag0, arrive(FARS))
-    for b in (0, 2, 1, 3):
-        mult(b, "f")
     bring("a", 0, "p")
     bring("v", 2, "p")
     bring("a", 1, "p")
     bring("v", 3, "p")
-    bring("a", 0, "f")
+    mult(0, "f0")
+    mult(0, "f1")
+    for b, run in ((2, "f"), (3, "g1"), (1, "f"), (3, "g0")):
+        mult(b, run)
+    bring("a", 0, "f0")
+    bring("v", 0, "f1")
+    bring("a", 3, "g1")
     bring("v", 2, "f")
     places(0)
     bring("v", 1, "f")
-    bring("v", 3, "f")
+    bring("v", 3, "g0")
     places(2)
     every(1)
     every(3)
@@ -450,7 +492,7 @@ def rank_program(g, core, T, topo):
     out("v", 2)
     out("a", 3)
     need("s", e_y)
-    g.wait_ge(T.sem.sentg, sent)
+    g.wait_ge(T.sem.sent, 2 * sent)
     for e in made:
         if not e["w"]:
             need("g", e)

import numpy as np
from concourse.bass import DstId, RemoteDMATransfer
from concourse.mybir import dt, AluOpType, ActivationFunctionType

N, NODES, CAP, F = 4, 128, 160, 8
SL = N * CAP
HF = 2 * CAP
UW = SL + 8
ST = 7
TR = ST * NODES
SCANNED = (1, 3)

SCRATCH = {
    "snl": ("sbuf", [128, SL // 16], "int32"), "nbl": ("sbuf", [128, 64], "int32"), "dnb": ("dram", [16, 64], "int32"),
    "two": ("sbuf", [128, 64], "int32"), "nbo": ("sbuf", [128, 64], "uint16"), "nbi": ("sbuf", [128, 16], "uint16"),
    "ill": ("sbuf", [128, 128], "int32"), "ilo": ("sbuf", [128, 128], "uint16"), "dil": ("dram", [16, 128], "int32"),
    "glo": ("sbuf", [128, 32], "uint16"), "gio": ("sbuf", [128, 32], "int32"),
    "pidx": ("sbuf", [128, 1], "int32"), "p12": ("sbuf", [128, 1], "int32"), "ppf": ("sbuf", [128, 1], "float32"),
    "uio": ("sbuf", [128, 8], "int32"), "ui7": ("sbuf", [128, 8], "int32"), "uno": ("sbuf", [128, 8], "uint16"),
    "vals": ("sbuf", [128, 256], "int32"), "inv": ("sbuf", [128, SL], "int32"),
    "iv": ("sbuf", [128, 80], "int32"), "ivm": ("sbuf", [128, 40], "int32"), "lt": ("sbuf", [128, 40], "uint16"),
    "xt": ("sbuf", [128, 512], "bfloat16"), "grt": ("sbuf", [128, 512], "bfloat16"),
    "wt": ("sbuf", [128, 2048], "bfloat16"), "w2t": ("sbuf", [128, 2048], "bfloat16"),
    "xg": ("sbuf", [128, 4 * SL], "bfloat16"), "gt": ("sbuf", [128, 4 * SL], "bfloat16"),
    "d0": ("sbuf", [128, 4 * TR], "bfloat16"), "d1": ("sbuf", [128, 4 * TR], "bfloat16"),
    "gb": ("sbuf", [128, 4 * TR], "bfloat16"),
    "rs": ("sbuf", [128, F * NODES], "bfloat16"),
    "zz": ("sbuf", [128, 4 * SL], "float32"), "zs": ("sbuf", [128, 4 * NODES], "float32"),
    "ma": ("sbuf", [128, 4 * NODES], "float32"), "mb": ("sbuf", [128, 4 * NODES], "float32"),
    "uu": ("sbuf", [128, 4 * UW], "float32"),
    "ps": ("psum", [128, 4096], "float32"),
}
for _i in range(4, 9):
    SCRATCH["nb%d" % _i] = ("sbuf", [128, 64], "int32")
for _n, _w in (("wq", 512), ("vq", 512), ("sx", SL), ("sg", SL), ("lx", SL), ("lg", SL)):
    SCRATCH[_n + "c"] = ("sbuf", [128, _w], "float8_e4m3fn_x4")
    SCRATCH[_n + "p"] = ("sbuf", [128, _w], "uint8")
for _b in range(4):
    SCRATCH["so%d" % _b] = ("sbuf", [128, SL // 16], "uint16")
    SCRATCH["yh%d" % _b] = ("sbuf", [128, 128], "float32")
    if _b in SCANNED:
        SCRATCH["ug%d" % _b] = ("sbuf", [128, F * NODES], "float32")
        SCRATCH["us%d" % _b] = ("sbuf", [128, F * NODES], "float32")
    else:
        for _k in range(4):
            SCRATCH["ac%d%d" % (_b, _k)] = ("sbuf", [128, 256], "float32")
    SCRATCH["yo%d" % _b] = ("sbuf", [128, 128], "float32")

EVENTS = 145
SEMAPHORES = ["ax0", "ax1", "ag0", "ag1", "sent"] + ["e%d" % _i for _i in range(EVENTS)]


def rank_program(g, core, T, topo):
    r = T.rank_of(core)
    if r is None:
        return
    A, Act = AluOpType, ActivationFunctionType
    cores = list(T.cores)
    Q = {"g": g, "v": g.vector, "a": g.scalar, "s": g.sync, "t": g.tensor}
    V, S, Y, TE = g.vector, g.scalar, g.sync, g.tensor

    pair = r - r % 2
    far = N // 2 - pair
    mate = pair + 1 - r % 2
    MATE, FARS = (mate,), (far, far + 1)
    OWN, PART, NEAR, FAR = CAP * r, CAP * mate, CAP * pair, CAP * far

    made, seen = [], set()

    def ev():
        e = {"k": len(made), "s": T.sem["e%d" % len(made)], "n": 0, "w": False}
        made.append(e)
        return e

    def inc(op, e, n=1):
        op.then_inc(e["s"], n)
        e["n"] += n
        return e

    def do(op):
        return inc(op, ev())

    def need(q, *es):
        for e in es:
            if (q, e["k"]) not in seen:
                seen.add((q, e["k"]))
                e["w"] = True
                Q[q].wait_ge(e["s"], e["n"])

    def send(src, dst, to, arrived):
        for part in (0, 1):
            tr = []
            for i, d in enumerate(to):
                rid, pid, _ = topo.addr(cores[d])
                es = topo.engines(cores[r], cores[d])[(part + i) % 2::2]
                a, b = CAP * d, CAP * r
                if part == 0:
                    f, t = T[src + "c"][:, a:a + CAP].bitcast(dt.uint8), T[dst + "c"][:, b:b + CAP].bitcast(dt.uint8)
                else:
                    f, t = T[src + "p"][:, a:a + CAP], T[dst + "p"][:, b:b + CAP]
                tr.append(RemoteDMATransfer(dst_ids=[DstId(rid=rid, pnc=pid)], dma_engine_mask=sum(1 << e for e in es),
                                            remote_sem=arrived, src=f, dst=t))
            g.remote_dma_fused(tr, local_sem=T.sem.sent)

    def arrive(at):
        return sum(len(topo.engines(cores[s], cores[r])) for s in at)

    sent = sum(len(topo.engines(cores[r], cores[d])) for d in MATE + FARS)

    e_x, e_sn, e_w, e_dnb, e_nb, e_gr, e_inv, e_iln = ev(), ev(), ev(), ev(), ev(), ev(), ev(), ev()
    for p in range(4):
        inc((Y, S)[p % 2].dma_start(T.snl[16 * p:16 * p + 16, :], T.sn[:, :]), e_sn, 16)
    inc(Y.dma_start(T.xt[:, :], T.x[:, :]), e_x, 16)
    for k in range(4):
        for h in range(2):
            inc((S, Y)[h].dma_start(T.dnb[:, 16 * k + 8 * h:16 * k + 8 * h + 8], T.nb[k:16:4, :]), e_dnb, 16)
    inc(Y.dma_start(T.wt[:, :], T.w[:, :]), e_w, 16)
    inc(Y.dma_start(T.grt[:, :], T.gr[:, :]), e_gr, 16)
    for h in range(2):
        inc(Y.dma_start(T.inv[64 * h:64 * h + 1, :], T.sn[:, :]), e_inv, 16)
    need("s", e_dnb)
    for p in range(4):
        inc(Y.dma_start(T.nbl[16 * p:16 * p + 16, :], T.dnb[:, :]), e_nb, 16)
    e_dil, e_w2 = ev(), ev()

    e_p, e_zero, e_p12, e_vals = ev(), ev(), ev(), ev()
    inc(g.iota(T.pidx[:, 0:1], [[1, 1]], 0, 129), e_p)
    e_gio = do(g.iota(T.gio[:, :], [[1, 4], [16, 8]], 0, 0))
    e_uio = do(g.iota(T.uio[:, :], [[1, 8]], 0, 8))
    inc(g.iota(T.two[:, :], [[0, 4], [SL, 2], [0, 8]], 0, 0), e_uio)
    inc(g.iota(T.vals[0:64, :], [[2, 2], [ST, NODES]], NODES + 4, 0), e_uio)
    need("g", e_p, e_gio, e_uio)
    inc(g.iota(T.vals[64:128, :], [[-1, 2], [ST, NODES]], NODES + 2, 0), e_vals)
    inc(V.memset(T.d1[:, 0:4 * TR:ST], 0.0), e_zero)
    need("v", e_p)
    inc(V.tensor_scalar(T.p12[:, 0:1], T.pidx[:, 0:1], 3 * 128 + 12, None, A.bitwise_and), e_p12)
    inc(V.memset(T.d0[:, 0:4 * TR:ST], 0.0), e_zero)
    need("v", e_p12)
    e_ppf = do(V.tensor_copy(T.ppf[:, 0:1], T.p12[:, 0:1]))
    inc(V.memset(T.d0[:, 4:4 * TR:ST], 0.0), e_zero)

    need("v", e_sn)
    e_so = [ev(), ev(), ev(), ev()]
    for t in (0, 2, 1, 3):
        for h in range(2):
            inc(V.tensor_scalar(T["so%d" % t][64 * h:64 * h + 64, :], T.snl[0:64, :], 4.0, float(t), A.mult, A.add), e_so[t])

    def copy(q, out, src, e):
        return inc(S.activation(out, src, Act.Copy) if q == "a" else V.tensor_copy(out, src), e)

    def pick(q, t, at, e, a=0, b=None):
        lo, hi = CAP * at[0] + a, CAP * at[0] + (b or CAP * len(at))
        copy(q, T.xg[:, 4 * lo + t:4 * hi:4], T.xt[:, 0:512].indirect(T["so%d" % t][:, lo // 16:hi // 16]), e)

    def pack(dst, src, at):
        a, b = CAP * at[0], CAP * (at[-1] + 1)
        return do(V.quantize_mx(T[dst + "c"][:, a:b], T[dst + "p"][:, a:b], T[src][:, 4 * a:4 * b]))

    need("a", e_x)
    need("v", e_x)
    e_g0, e_g1 = ev(), ev()
    for q, ts in (("a", (0, 1)), ("v", (2, 3))):
        for t in ts:
            need(q, e_so[t])
            pick(q, t, MATE, e_g0)
    for t in (0, 1):
        pick("a", t, FARS, e_g1)
    pick("v", 2, FARS, e_g1, 0, CAP)
    need("v", e_g0)
    need("g", pack("sx", "xg", MATE))
    send("sx", "lx", MATE, T.sem.ax0)
    pick("v", 2, FARS, e_g1, CAP, HF)
    pick("v", 3, FARS, e_g1)
    need("v", e_ppf, e_gio)
    e_glo = do(V.tensor_scalar(T.glo[:, :], T.gio[:, :], T.ppf[:, 0:1], None, A.add))
    inc(V.memset(T.d0[:, 6:3 * TR:ST], 0.0), e_zero)
    need("v", e_g1)
    need("g", pack("sx", "xg", FARS))
    send("sx", "lx", FARS, T.sem.ax1)

    e_xo = ev()
    for t in range(4):
        need("a", e_so[t])
        pick("a", t, (r,), e_xo)
    e_ch = {}
    need("a", e_gr, e_glo)
    e_gp1 = copy("a", T.d0[:, 1:4 * TR:ST], T.grt[:, 0:512].indirect(T.glo[:, 0:32]), ev())
    need("v", e_nb, e_uio)
    e_4 = do(V.tensor_scalar(T.nb4[0:64, :], T.nbl[0:64, :], 4, None, A.arith_shift_right))
    inc(V.tensor_tensor(T.nb8[0:64, :], T.nbl[0:64, :], T.two[0:64, :], A.add), e_4)
    e_56 = do(V.tensor_scalar(T.nb5[0:64, :], T.nbl[0:64, :], 40.0, None, A.mult))
    inc(V.memset(T.d0[:, 3 * TR + 6:4 * TR:ST], 0.0), e_zero)
    e_uz = inc(V.memset(T.uu[:, 0:4 * UW:UW], 0.0), e_zero)
    need("v", e_4)
    inc(V.tensor_scalar(T.nb6[0:64, :], T.nb4[0:64, :], -639.0, None, A.mult), e_56)
    e_nbo = ev()
    for h in range(2):
        inc(V.tensor_copy(T.nbo[64 * h:64 * h + 64, :], T.nb8[0:64, :]), e_nbo)
    need("v", e_w)
    e_wq = do(V.quantize_mx(T.wqc[:, 0:256], T.wqp[:, 0:256], T.wt[:, 0:1024]))
    need("v", e_56)
    e = do(V.tensor_tensor(T.nb7[0:64, :], T.nb5[0:64, :], T.nb6[0:64, :], A.add))
    need("v", e_xo)
    e_xoq = pack("lx", "xg", (r,))
    need("v", e)
    e = ev()
    for h in range(2):
        inc(V.tensor_copy(T.nbi[64 * h:64 * h + 64, :], T.nb7[0:64, 32 * h + 8:32 * h + 24]), e)
    e_wq2 = do(V.quantize_mx(T.wqc[:, 256:512], T.wqp[:, 256:512], T.wt[:, 1024:2048]))
    e_d0 = [ev(), ev()]
    need("g", e_vals, e_gp1)
    for h in range(2):
        lo, hi = 2 * TR * h, 2 * TR * (h + 1)
        for step in (2, 3, 5):
            inc(g.affine_select(T.d0[:, lo + step:hi:ST], T.d0[:, lo + 1:hi:ST], [[0, 2 * NODES]], A.is_ge, 0.0, 0, 0), e_d0[h])
    e_rs = do(g.iota(T.rs[:, :], [[0, F * NODES]], 1, 0, allow_small_or_imprecise_dtypes=True))
    need("g", e_rs)
    inc(g.iota(T.rs[:, 0:F * NODES:F], [[0, NODES]], 0, 0, allow_small_or_imprecise_dtypes=True), e_rs)
    need("v", e, e_uio, e_vals, e_inv)
    e_sc = do(V.tensor_copy(T.inv[:, 0:SL].indirect(T.nbi[:, 0:16]), T.vals[:, 0:256]))
    e_iv = ev()
    need("s", e_sc)
    for p in range(4):
        for h in range(2):
            inc(Y.dma_start(T.iv[16 * p:16 * p + 16, 40 * h:40 * h + 40], T.inv[64 * h:64 * h + 1, :]), e_iv, 16)

    last = {}

    def product(st, mv, b, bank, a, n):
        if bank in last:
            need("t", last[bank])
        return do(TE.matmul_mx(T.ps[:, 512 * bank:512 * bank + n], T[st + "c"][:, 128 * b:128 * b + 128], T[st + "p"][:, 128 * b:128 * b + 128],
                               T[mv + "c"][:, a:a + n], T[mv + "p"][:, a:a + n], True, True))

    def take(q, bank, out, n, e_mm):
        need(q, e_mm)
        last[bank] = copy(q, out, T.ps[:, 512 * bank:512 * bank + n], ev())
        return last[bank]

    need("t", e_wq, e_xoq)
    TE.wait_ge(T.sem.ax0, arrive(MATE))
    e_m = {}
    for b in (0, 1):
        e_m[b, 0] = product("wq", "lx", b, b, NEAR, HF)
    TE.wait_ge(T.sem.ax1, arrive(FARS))
    e_m[0, 1] = product("wq", "lx", 0, 4, FAR, CAP)
    e_m[0, 2] = product("wq", "lx", 0, 7, FAR + CAP, CAP)
    e_m[1, 1] = product("wq", "lx", 1, 5, FAR, HF)
    need("t", e_wq2)
    for b, late in ((2, 1), (2, 0), (3, 0)):
        e_m[b, late] = product("wq", "lx", b, b + 4 * late, FAR if late else NEAR, HF)
    need("s", e_m[0, 1])
    inc(Y.dma_start(T.w2t[:, :], T.w2[:, :]), e_w2, 16)
    for f in range(F):
        inc(Y.dma_start(T.dil[:, 8 * f:8 * f + 8], T.il[f:16:F, :]), e_dil, 16)
    inc(Y.dma_start(T.dil[:, 64:128], T.il[:, :]), e_dil, 16)
    need("s", e_dil)
    for p in range(4):
        inc(Y.dma_start(T.ill[16 * p:16 * p + 16, :], T.dil[:, :]), e_iln, 16)

    e_z = {b: [] for b in range(4)}
    e_zs, e_ma, e_mb, e_p2, e_w3, e_k = ({b: [] for b in range(4)} for _ in range(6))

    def nbr(bs, k):
        return T.zz[:, SL * bs[0]:SL * (bs[-1] + 1)].indirect(T.nbo[:, 16 * k:16 * k + 8 * len(bs)])

    def node(name, bs):
        return T[name][:, NODES * bs[0]:NODES * (bs[-1] + 1)]

    def mask(bs, step):
        return T.d1[:, TR * bs[0] + step:TR * (bs[-1] + 1):ST]

    def after(q, d, bs):
        for b in bs:
            need(q, *d[b])

    def gave(d, bs, *ops):
        e = ev()
        for op in ops:
            inc(op, e)
        for b in bs:
            d[b].append(e)

    def zcopy(q, b, late):
        a = SL * b + (FAR if late else NEAR)
        e_z[b].append(take(q, b + 4 * late, T.zz[:, a:a + HF], HF, e_m[b, late]))

    def zs(*bs):
        need("a", e_nbo)
        after("a", e_z, bs)
        gave(e_zs, bs, S.activation(node("zs", bs), nbr(bs, 1), Act.Copy))

    def m01(*bs):
        need("v", e_nbo)
        after("v", e_zs, bs)
        after("v", e_z, bs)
        gave(e_ma, bs, V.tensor_tensor(node("ma", bs), nbr(bs, 0), node("zs", bs), A.max))

    def q0(*bs):
        gave(e_k, bs, V.tensor_tensor(mask(bs, 4), nbr(bs, 0), node("zs", bs), A.is_ge))

    def m012(*bs):
        after("v", e_ma, bs)
        gave(e_mb, bs, V.tensor_tensor(node("mb", bs), nbr(bs, 2), node("ma", bs), A.max))

    def p2(*bs):
        after("v", e_ma, bs)
        gave(e_p2, bs, V.tensor_tensor(mask(bs, 2), nbr(bs, 2), node("ma", bs), A.is_gt))

    def w3(*bs):
        after("v", e_mb, bs)
        gave(e_w3, bs, V.tensor_tensor(mask(bs, 1), nbr(bs, 3), node("mb", bs), A.is_gt))

    def affine(q, bs, to, src, scale, bias):
        if q == "a":
            return S.activation(mask(bs, to), mask(bs, src), Act.Identity, bias=bias, scale=scale)
        return V.tensor_scalar(mask(bs, to), mask(bs, src), scale, bias, A.mult, A.add)

    def n2(q, *bs):
        after(q, e_p2, bs)
        gave(e_k, bs, affine(q, bs, 6, 2, -1.0, 1.0))

    def n3(q, *bs):
        after(q, e_w3, bs)
        gave(e_k, bs, affine(q, bs, 3, 1, 1.0, -1.0), affine(q, bs, 5, 1, 1.0, -1.0))

    def ch(b):
        need("v", e_zero, e_d0[b // 2], *e_k[b])
        e_ch[b] = do(V.tensor_tensor_scan(T.gb[:, TR * b:TR * b + TR], T.d0[:, TR * b:TR * b + TR], T.d1[:, TR * b:TR * b + TR], 0.0, A.subtract, A.mult))

    def grad(q, b, lo, hi, e):
        need(q, e_lt, e_ch[b])
        copy(q, T.gt[:, 4 * lo + b:4 * hi:4], T.gb[:, TR * b:TR * b + TR].indirect(T.lt[:, lo // 16:hi // 16]), e)

    e_gf, e_gp, e_go, e_gf0 = ev(), ev(), ev(), ev()
    zcopy("a", 0, 0)
    zcopy("a", 1, 0)
    e_z[0].append(take("a", 4, T.zz[:, FAR:FAR + CAP], CAP, e_m[0, 1]))
    e_z[0].append(take("v", 7, T.zz[:, FAR + CAP:FAR + HF], CAP, e_m[0, 2]))
    e_m[3, 1] = product("wq", "lx", 3, 7, FAR, HF)
    zcopy("v", 1, 1)
    zcopy("v", 2, 1)
    zs(0)
    zs(1)
    for b, late in ((2, 0), (3, 0), (3, 1)):
        zcopy("a", b, late)
    zs(2, 3)
    for b in (0, 1):
        m01(b)
        q0(b)
    m012(0, 1)
    p2(0, 1)
    w3(0, 1)
    n2("a", 0, 1)
    m01(2, 3)
    n3("a", 0)
    n3("a", 1)
    need("v", e_iv)
    e = do(V.tensor_tensor(T.ivm[0:64, :], T.iv[0:64, 0:40], T.iv[0:64, 40:80], A.max))
    q0(2, 3)
    need("v", e)
    e_lt = ev()
    for h in range(2):
        inc(V.tensor_scalar(T.lt[64 * h:64 * h + 64, :], T.ivm[0:64, :], -float(NODES), None, A.add), e_lt)
    ch(0)
    grad("a", 0, 0, SL, e_gf0)
    m012(2, 3)
    p2(2, 3)
    ch(1)
    n2("a", 2, 3)
    w3(2)
    grad("a", 1, 0, SL, e_gf0)
    w3(3)
    n3("v", 2)
    n3("v", 3)
    ch(2)
    grad("a", 2, FAR, FAR + HF, e_gf)
    ch(3)
    grad("v", 2, PART, PART + CAP, e_gp)
    grad("v", 3, PART, PART + CAP, e_gp)
    grad("a", 3, FAR, FAR + HF - 64, e_gf)
    grad("v", 3, FAR + HF - 64, FAR + HF, e_gf)
    need("v", e_w2)
    e_vq = do(V.quantize_mx(T.vqc[:, 0:128], T.vqp[:, 0:128], T.w2t[:, 0:512]))
    need("v", e_gf0, e_gp)
    need("g", pack("sg", "gt", MATE))
    send("sg", "lg", MATE, T.sem.ag1)
    need("v", e_gf)
    need("g", pack("sg", "gt", FARS))
    send("sg", "lg", FARS, T.sem.ag0)

    for b in (2, 3):
        grad("a", b, OWN, OWN + CAP, e_go)
    inc(V.quantize_mx(T.vqc[:, 128:512], T.vqp[:, 128:512], T.w2t[:, 512:2048]), e_vq)
    need("v", e_go)
    e_goq = pack("lg", "gt", (r,))
    need("v", e_uio)
    e = do(V.tensor_scalar(T.ui7[:, :], T.uio[:, :], 127, None, A.bitwise_and))
    need("v", e_iln)
    e_ilo = ev()
    for h in range(2):
        inc(V.tensor_scalar(T.ilo[64 * h:64 * h + 64, :], T.ill[0:64, :], 1.0, None, A.add), e_ilo)
    need("v", e)
    e_uno = do(V.tensor_copy(T.uno[:, :], T.ui7[:, :]))

    e_u = {b: [e_uz] for b in range(4)}
    e_ac, e_ug, e_us, e_yh, e_y = {}, {}, {}, {}, ev()
    RUN = {"o": (OWN, CAP, 0), "f": (FAR, HF, 0), "p": (PART, CAP, 4), "f0": (FAR, CAP, 0), "f1": (FAR + CAP, CAP, 4),
           "g0": (FAR, HF - 128, 0), "g1": (FAR + HF - 128, 128, 2)}

    def mult(b, run):
        a, n, bank = RUN[run]
        e_m[b, run] = product("vq", "lg", b, bank + b, a, n)

    def win(b):
        return T.uu[:, UW * b:UW * b + SL + 1]

    def bring(q, b, run):
        a, n, bank = RUN[run]
        e_u[b].append(take(q, bank + b, T.uu[:, UW * b + 1 + a:UW * b + 1 + a + n], n, e_m[b, run]))

    def places(b):
        need("a", e_ilo, *e_u[b])
        e_ac[b] = do(S.activation(T["ac%d0" % b][:, :], win(b).indirect(T.ilo[:, 48:64]), Act.Copy))

    def every(b):
        need("a", e_ilo, *e_u[b])
        e_ug[b] = do(S.activation(T["ug%d" % b][:, :], win(b).indirect(T.ilo[:, 64:128]), Act.Copy))

    def add(b, i):
        need("v", e_ilo, e_ac[b], *e_u[b])
        e_ac[b] = do(V.tensor_tensor(T["ac%d%d" % (b, i + 1)][:, :], win(b).indirect(T.ilo[:, 16 * i:16 * i + 16]), T["ac%d%d" % (b, i)][:, :], A.add))

    def scan(b):
        need("v", e_rs, e_ug[b])
        e_us[b] = do(V.tensor_tensor_scan(T["us%d" % b][:, :], T.rs[:, :], T["ug%d" % b][:, :], 0.0, A.mult, A.add))

    def half(q, b):
        need(q, e_uno, e_ac[b])
        e_yh[b] = copy(q, T["yh%d" % b][:, :], T["ac%d3" % b][:, 128:256].indirect(T.uno[:, :]), ev())

    def out(q, b):
        e = ev()
        if b in SCANNED:
            need(q, e_us[b])
            copy(q, T["yo%d" % b][:, :], T["us%d" % b][:, F - 1:F * NODES:F], e)
        else:
            need(q, e_ac[b], e_yh[b])
            inc(V.tensor_tensor(T["yo%d" % b][:, :], T["ac%d3" % b][:, 0:128].indirect(T.uno[:, :]), T["yh%d" % b][:, :], A.add), e)
        dq = "a" if b == 3 else "s"
        need(dq, e)
        inc(Q[dq].dma_start(T.y[:, 128 * b:128 * b + 128], T["yo%d" % b][:, :]), e_y, 16)

    need("t", e_vq, e_goq)
    for b in (0, 2, 1, 3):
        mult(b, "o")
    bring("a", 0, "o")
    bring("v", 2, "o")
    bring("a", 1, "o")
    bring("v", 3, "o")
    TE.wait_ge(T.sem.ag1, arrive(MATE))
    for b in (0, 2, 1, 3):
        mult(b, "p")
    TE.wait_ge(T.sem.ag0, arrive(FARS))
    bring("a", 0, "p")
    bring("v", 2, "p")
    bring("a", 1, "p")
    bring("v", 3, "p")
    mult(0, "f0")
    mult(0, "f1")
    for b, run in ((2, "f"), (3, "g1"), (1, "f"), (3, "g0")):
        mult(b, run)
    bring("a", 0, "f0")
    bring("v", 0, "f1")
    bring("a", 3, "g1")
    bring("v", 2, "f")
    places(0)
    bring("v", 1, "f")
    bring("v", 3, "g0")
    places(2)
    every(1)
    every(3)
    for i in range(3):
        add(0, i)
        add(2, i)
    half("a", 0)
    half("a", 2)
    scan(1)
    scan(3)
    out("a", 1)
    out("v", 0)
    out("v", 2)
    out("a", 3)
    need("s", e_y)
    g.wait_ge(T.sem.sent, 2 * sent)
    for e in made:
        if not e["w"]:
            need("g", e)
